import numpy as np
import ml_dtypes


def mxq(x, axis, fmt="e4m3"):
    dtype, down = {"e4m3": (ml_dtypes.float8_e4m3fn, 7), "e5m2": (ml_dtypes.float8_e5m2, 14)}[fmt]
    v = np.moveaxis(np.asarray(x, np.float32).astype(ml_dtypes.bfloat16).astype(np.float64), axis, -1)
    blocks = v.reshape(v.shape[:-1] + (-1, 32))
    amax = np.abs(blocks).max(-1, keepdims=True)
    byte = np.maximum(np.where(amax > 0, np.frexp(amax)[1] - 1 + 127, 0) - down, 1)
    scale = np.exp2(byte - 127.0)
    codes = (blocks / scale).astype(np.float32).astype(dtype).astype(np.float64)
    return np.moveaxis((codes * scale).reshape(v.shape), -1, axis)


WIDE = False


def mx_kscale(k):
    if not WIDE:
        return np.ones(k)
    levels = np.array([10, -10, 5, -5, 0])
    if k % 512:
        return np.exp2(np.random.permutation(np.resize(levels, k // 32))).repeat(32)
    a = np.empty((k // 512, 16))
    for p in range(k // 512):
        a[p, :8] = np.random.permutation(np.resize(levels, 8))
        for g in range(8):
            far = levels[np.abs(levels - a[p, g]) >= 10]
            a[p, g + 8] = far[np.random.randint(len(far))]
    return np.exp2(a.ravel()).repeat(32)


def f64(x):
    return np.asarray(x).astype(np.float64)


def striped(idx):
    return np.tile(idx.reshape(-1, 16).T, (8, 1)).astype(np.uint16)


def unstriped(offs):
    return offs[:16].T.reshape(-1).astype(np.int64)


E2M1 = np.array([0.0, 0.5, 1.0, 1.5, 2.0, 3.0, 4.0, 6.0, -0.0, -0.5, -1.0, -1.5, -2.0, -3.0, -4.0, -6.0])


def pack_weight(w, fmt):
    k, n = w.shape
    w = f64(np.asarray(w, np.float32).astype(ml_dtypes.bfloat16)).reshape(k // 32, 32, n)
    amax = np.abs(w).max(1)
    if fmt == "e4m3":
        byte = np.frexp(amax)[1] - 1 + 127 - 7
    else:
        mant, ex = np.frexp(amax / 6.0)
        byte = np.where(mant > 0.5, ex, ex - 1) + 127
    byte = np.clip(np.where(amax > 0, byte, 1), 1, 254)
    scaled = (w * np.exp2(127.0 - byte)[:, None, :]).reshape(k, n).astype(np.float32)
    by_word = np.ascontiguousarray(scaled.reshape(k // 512, 128, 4, n).transpose(0, 1, 3, 2))
    if fmt == "e4m3":
        words = by_word.astype(ml_dtypes.float8_e4m3fn).view(np.uint8)
    else:
        c = by_word.astype(ml_dtypes.float4_e2m1fn).view(np.uint8) & 0xF
        words = (c[..., 0::2] | (c[..., 1::2] << 4)).reshape(k // 512, 128, 2 * n)
    return np.ascontiguousarray(words), np.ascontiguousarray(byte.astype(np.uint8).reshape(k // 512, 16, n))


def unpack_weight(words, scales, fmt):
    g, _, n = scales.shape
    words = np.ascontiguousarray(words).reshape(g, 128, n, -1)
    if fmt == "e4m3":
        vals = words.view(ml_dtypes.float8_e4m3fn).astype(np.float64)
    else:
        nib = np.empty((g, 128, n, 4), np.uint8)
        nib[..., 0::2] = words & 0xF
        nib[..., 1::2] = words >> 4
        vals = E2M1[nib]
    vals = vals * np.repeat(np.exp2(scales.astype(np.float64) - 127.0), 8, axis=1)[..., None]
    return vals.transpose(0, 1, 3, 2).reshape(g * 512, n)


def relu(v):
    return np.maximum(v, 0.0)


K, T, E, C, N = 1024, 1536, 4, 256, 128
K8 = 512


def by_expert(wq, xq):
    return np.concatenate([wq[e].T @ xq[:, e * C:(e + 1) * C] for e in range(E)], axis=1)


def setup_inputs():
    n = np.random.standard_normal
    s = mx_kscale(K)[:, None]
    w = n((E, K, N)) / np.sqrt(K) / s[None]
    w8 = [pack_weight(m[:K8], "e4m3") for m in w]
    w4 = [pack_weight(m[K8:], "e2m1") for m in w]
    return {
        "xT": (n((K, T)) * s).astype(np.float32),
        "xr": n((N, T)).astype(np.float32),
        "w8_words": np.stack([m[0] for m in w8]),
        "w8_scales": np.stack([m[1] for m in w8]),
        "w4_words": np.stack([m[0] for m in w4]),
        "w4_scales": np.stack([m[1] for m in w4]),
        "b": (0.3 * n((N, E))).astype(np.float32),
        "gate": np.tile(np.random.uniform(0.2, 1.0, E * C), (N, 1)).astype(np.float32),
        "offs": striped(np.random.permutation(T)[:E * C]),
    }


def reference(xT, xr, w8_words, w8_scales, w4_words, w4_scales, b, gate, offs):
    idx = unstriped(offs)
    w = np.stack([np.concatenate([unpack_weight(w8_words[e], w8_scales[e], "e4m3"), unpack_weight(w4_words[e], w4_scales[e], "e2m1")]) for e in range(E)])
    xq = mxq(f64(xT)[:, idx], 0, "e4m3")
    y = by_expert(w, xq)
    y = relu(y + np.repeat(f64(b), C, axis=1))
    out = f64(xr).copy()
    out[:, idx] += f64(gate) * y
    return out

@@ -1,0 +1,164 @@
+from contextlib import ExitStack
+
+import concourse.mybir as mybir
+
+F32 = mybir.dt.float32
+BF16 = mybir.dt.bfloat16
+I32 = mybir.dt.int32
+U32 = mybir.dt.uint32
+U16 = mybir.dt.uint16
+U8 = mybir.dt.uint8
+FP8X4 = mybir.dt.float8_e4m3fn_x4
+FP4X4 = mybir.dt.float4_e2m1fn_x4
+MULT = mybir.AluOpType.mult
+ADD = mybir.AluOpType.add
+COPY = mybir.ActivationFunctionType.Copy
+RELU = mybir.ActivationFunctionType.Relu
+
+P = 128
+K, T, E, C, N = 1024, 1536, 4, 256, 128
+PASS = 512
+FLOPS = 2 * E * C * K * N
+
+CHUNKS = (
+    (0, 0, 512, 160),
+    (0, 512, 512, 160),
+    (0, 1024, 512, 144),
+    (1, 0, 512, 512),
+    (1, 512, 512, 256),
+    (1, 1024, 256, 128),
+    (1, 1280, 256, 64),
+)
+
+CUTS = ((0, 512), (512, 1024), (1024, 1536))
+
+
+def tile_moe_res_lin_relu_kernel(
+    tc, xT, xr, w8_words, w8_scales, w4_words, w4_scales, b, gate, offs, out
+):
+    nc = tc.nc
+    with ExitStack() as ctx:
+        keep = ctx.enter_context(tc.tile_pool(name="keep", bufs=1))
+        psum = ctx.enter_context(tc.psum_pool(name="psum", bufs=1))
+
+        offsets = keep.tile([P, E * C // 16], U16, name="offsets")
+        raws = [keep.tile([P, 4, w], F32, name=f"raw{i}", align_bytes=64) for i, (a, c0, w, s) in enumerate(CHUNKS)]
+        groups = [keep.tile([P, w, 4], BF16, name=f"grp{i}", align_bytes=64) for i, (a, c0, w, s) in enumerate(CHUNKS)]
+        words = [keep.tile([P, T], U32, name=f"words{a}", align_bytes=64) for a in range(2)]
+        planes = keep.tile([P, T], U8, name="planes", align_bytes=64)
+        slot_words = [keep.tile([P, E * C], U32, name=f"slot_words{a}", align_bytes=64) for a in range(2)]
+        slot_planes = keep.tile([P, E * C], U8, name="slot_planes", align_bytes=64)
+        w8 = keep.tile([P, E, 4 * N], U8, name="w8", align_bytes=64)
+        w4 = keep.tile([P, E, 2 * N], U8, name="w4", align_bytes=64)
+        w_planes = keep.tile([P, E, N], U8, name="w_planes", align_bytes=64)
+        bias = keep.tile([P, E], F32, name="bias")
+        gates = keep.tile([P, E * C], F32, name="gates")
+        resid = keep.tile([P, T], F32, name="resid")
+        ys = [keep.tile([P, 2 * C], F32, name=f"y{g}") for g in range(2)]
+        routed = keep.tile([P, T], F32, name="routed")
+        sums = [keep.tile([P, hi - lo], F32, name=f"sum{i}") for i, (lo, hi) in enumerate(CUTS)]
+        banks = [psum.tile([P, C], F32, name=f"bank{e}") for e in range(E)]
+
+        nc.vector.memset(w_planes[:].rearrange("p e n -> p (e n)").bitcast(I32), 0)
+        nc.gpsimd.memset(planes[:], 0)
+        nc.vector.memset(routed[:], 0.0)
+
+        def load_x(i):
+            a, c0, w, s = CHUNKS[i]
+            src = xT[PASS * a : PASS * (a + 1), c0 : c0 + w].rearrange("(p j) w -> p j w", j=4)
+            nc.sync.dma_start(raws[i][:], src)
+
+        def load_planes(first, scales):
+            for q in range(4):
+                nc.sync.dma_start(
+                    w_planes[32 * q + first : 32 * q + first + 4, :, :].bitcast(I32),
+                    scales[:, 0, 4 * q : 4 * q + 4, :].rearrange("e q n -> q e n").bitcast(I32),
+                )
+
+        load_x(0)
+        load_x(1)
+        nc.sync.dma_start(offsets[:], offs)
+        for i in range(2, len(CHUNKS)):
+            load_x(i)
+        nc.sync.dma_start(w8[:].bitcast(I32), w8_words.rearrange("e a p n t -> p (e a) (n t)").bitcast(I32))
+        nc.sync.dma_start(w4[:].bitcast(I32), w4_words.rearrange("e a p m -> p (e a) m").bitcast(I32))
+        nc.sync.dma_start(bias[:], b)
+        load_planes(4, w8_scales)
+        load_planes(0, w4_scales)
+        nc.sync.dma_start(gates[:], gate)
+        nc.sync.dma_start(resid[:], xr)
+
+        def cast(i):
+            a, c0, w, s = CHUNKS[i]
+            for engine_copy, lo, hi in ((scalar_copy, 0, s), (nc.vector.tensor_copy, s, w)):
+                if hi > lo:
+                    engine_copy(
+                        groups[i][:, lo:hi, :].rearrange("p (c i) j -> p c j i", i=4),
+                        raws[i][:, :, lo:hi].rearrange("p j (c i) -> p c j i", i=4),
+                    )
+
+        def scalar_copy(dst, src):
+            nc.scalar.activation(dst, src, COPY)
+
+        def quantise(i):
+            a, c0, w, s = CHUNKS[i]
+            first = 4 if a == 0 else 0
+            nc.vector.quantize_mx(
+                out=words[a][:, c0 : c0 + w].bitcast(FP8X4),
+                scales=planes[first:P, c0 : c0 + w],
+                in_=groups[i][:].rearrange("p w j -> p (w j)"),
+            )
+
+        def gather_words(a, lo, hi):
+            nc.vector.tensor_copy(slot_words[a][:, lo:hi], words[a][:].indirect(offsets[:, lo // 16 : hi // 16]))
+
+        def gather_planes(lo, hi):
+            nc.vector.tensor_copy(slot_planes[:, lo:hi], planes[:].indirect(offsets[:, lo // 16 : hi // 16]))
+
+        def multiply(e):
+            for h in range(C // 128):
+                cols = slice(e * C + h * 128, e * C + (h + 1) * 128)
+                acc = banks[e][:, h * 128 : (h + 1) * 128]
+                nc.tensor.matmul_mx(
+                    out=acc,
+                    lhsT=w8[:, e, :].bitcast(FP8X4),
+                    lhsT_scale=w_planes[4:P, e, :],
+                    rhs=slot_words[0][:, cols].bitcast(FP8X4),
+                    rhs_scale=slot_planes[4:P, cols],
+                    start=True,
+                    stop=False,
+                )
+                nc.tensor.matmul_mx(
+                    out=acc,
+                    lhsT=w4[:, e, :].bitcast(FP4X4),
+                    lhsT_scale=w_planes[:, e, :],
+                    rhs=slot_words[1][:, cols].bitcast(FP8X4),
+                    rhs_scale=slot_planes[:, cols],
+                    start=False,
+                    stop=True,
+                )
+            nc.scalar.activation(ys[e // 2][:, (e % 2) * C : (e % 2 + 1) * C], banks[e][:], RELU, bias=bias[:, e : e + 1])
+
+        n = len(CHUNKS)
+        for i in range(n):
+            if i == 3:
+                quantise(2)
+                gather_words(0, 0, E * C)
+            cast(i)
+            if i >= 1 and i != 3:
+                quantise(i - 1)
+        quantise(n - 1)
+        for g in range(2):
+            gather_words(1, g * 512, (g + 1) * 512)
+            gather_planes(g * 512, (g + 1) * 512)
+            for e in (2 * g, 2 * g + 1):
+                multiply(e)
+        for g in range(2):
+            nc.vector.tensor_tensor(
+                routed[:].indirect(offsets[:, g * 32 : (g + 1) * 32]), ys[g][:], gates[:, g * 512 : (g + 1) * 512], MULT
+            )
+
+        for i, (lo, hi) in enumerate(CUTS):
+            cols = slice(lo, hi)
+            nc.vector.tensor_tensor(sums[i][:], routed[:, cols], resid[:, cols], ADD)
+            nc.sync.dma_start(out[:, cols], sums[i][:])

@@ -17,19 +17,18 @@ RELU = mybir.ActivationFunctionType.Relu
 
 P = 128
 K, T, E, C, N = 1024, 1536, 4, 256, 128
+S = E * C
 PASS = 512
 FLOPS = 2 * E * C * K * N
 
-CHUNKS = (
-    (0, 0, 512, 160),
-    (0, 512, 512, 160),
-    (0, 1024, 512, 144),
-    (1, 0, 512, 512),
-    (1, 512, 512, 256),
-    (1, 1024, 256, 128),
-    (1, 1280, 256, 64),
+PIECES = (
+    ((0, 512, 512), (512, 768, 256), (1280, 256, 96)),
+    ((0, 512, 512), (512, 512, 512), (1024, 512, 224)),
+    ((0, 512, 512), (512, 512, 512), (1024, 512, 512)),
+    ((0, 512, 512), (512, 512, 512), (1024, 512, 320)),
 )
 
+SCATTERS = ((0, 1), (1, 4))
 CUTS = ((0, 512), (512, 1024), (1024, 1536))
 
 
@@ -41,90 +40,97 @@ def tile_moe_res_lin_relu_kernel(
         keep = ctx.enter_context(tc.tile_pool(name="keep", bufs=1))
         psum = ctx.enter_context(tc.psum_pool(name="psum", bufs=1))
 
-        offsets = keep.tile([P, E * C // 16], U16, name="offsets")
-        raws = [keep.tile([P, 4, w], F32, name=f"raw{i}", align_bytes=64) for i, (a, c0, w, s) in enumerate(CHUNKS)]
-        groups = [keep.tile([P, w, 4], BF16, name=f"grp{i}", align_bytes=64) for i, (a, c0, w, s) in enumerate(CHUNKS)]
-        words = [keep.tile([P, T], U32, name=f"words{a}", align_bytes=64) for a in range(2)]
-        planes = keep.tile([P, T], U8, name="planes", align_bytes=64)
-        slot_words = [keep.tile([P, E * C], U32, name=f"slot_words{a}", align_bytes=64) for a in range(2)]
-        slot_planes = keep.tile([P, E * C], U8, name="slot_planes", align_bytes=64)
+        offsets = keep.tile([P, S // 16], U16, name="offsets")
+        raws = [
+            [keep.tile([P, 2, w], F32, name=f"raw{u}_{i}", align_bytes=64) for i, (c0, w, s) in enumerate(PIECES[u])]
+            for u in range(4)
+        ]
+        pairs = [keep.tile([P, T, 2], BF16, name=f"pairs{u}", align_bytes=64) for u in range(4)]
+        picked1 = keep.tile([P, E, 2, C], U32, name="picked1", align_bytes=64)
+        woven0 = keep.tile([P, S, 2], U32, name="woven0", align_bytes=64)
+        woven1 = [keep.tile([P, C, 2], U32, name=f"woven1_{e}", align_bytes=64) for e in range(E)]
+        codes0 = keep.tile([P, S], U32, name="codes0", align_bytes=64)
+        scales0 = keep.tile([P, S], U8, name="scales0", align_bytes=64)
+        codes1 = [keep.tile([P, C], U32, name=f"codes1_{e}", align_bytes=64) for e in range(E)]
+        scales1 = [keep.tile([P, C], U8, name=f"scales1_{e}", align_bytes=64) for e in range(E)]
         w8 = keep.tile([P, E, 4 * N], U8, name="w8", align_bytes=64)
         w4 = keep.tile([P, E, 2 * N], U8, name="w4", align_bytes=64)
         w_planes = keep.tile([P, E, N], U8, name="w_planes", align_bytes=64)
         bias = keep.tile([P, E], F32, name="bias")
-        gates = keep.tile([P, E * C], F32, name="gates")
+        gates = keep.tile([P, S], F32, name="gates")
         resid = keep.tile([P, T], F32, name="resid")
-        ys = [keep.tile([P, 2 * C], F32, name=f"y{g}") for g in range(2)]
+        ys = [keep.tile([P, (hi - lo) * C], F32, name=f"y{g}") for g, (lo, hi) in enumerate(SCATTERS)]
         routed = keep.tile([P, T], F32, name="routed")
         sums = [keep.tile([P, hi - lo], F32, name=f"sum{i}") for i, (lo, hi) in enumerate(CUTS)]
         banks = [psum.tile([P, C], F32, name=f"bank{e}") for e in range(E)]
 
-        nc.vector.memset(w_planes[:].rearrange("p e n -> p (e n)").bitcast(I32), 0)
-        nc.gpsimd.memset(planes[:], 0)
+        nc.gpsimd.memset(w_planes[:].rearrange("p e n -> p (e n)").bitcast(I32), 0)
         nc.vector.memset(routed[:], 0.0)
 
-        def load_x(i):
-            a, c0, w, s = CHUNKS[i]
+        def load_x(u, i):
+            c0, w, s = PIECES[u][i]
+            a, h = divmod(u, 2)
             src = xT[PASS * a : PASS * (a + 1), c0 : c0 + w].rearrange("(p j) w -> p j w", j=4)
-            nc.sync.dma_start(raws[i][:], src)
+            nc.sync.dma_start(raws[u][i][:], src[:, 2 * h : 2 * h + 2, :])
 
-        def load_planes(first, scales):
-            for q in range(4):
-                nc.sync.dma_start(
-                    w_planes[32 * q + first : 32 * q + first + 4, :, :].bitcast(I32),
-                    scales[:, 0, 4 * q : 4 * q + 4, :].rearrange("e q n -> q e n").bitcast(I32),
-                )
+        def load_plane(r):
+            first, scales = ((4, w8_scales), (0, w4_scales))[r // 4]
+            q = r % 4
+            nc.sync.dma_start(
+                w_planes[32 * q + first : 32 * q + first + 4, :, :].bitcast(I32),
+                scales[:, 0, 4 * q : 4 * q + 4, :].rearrange("e q n -> q e n").bitcast(I32),
+            )
 
-        load_x(0)
-        load_x(1)
+        load_x(0, 0)
+        load_x(0, 1)
         nc.sync.dma_start(offsets[:], offs)
-        for i in range(2, len(CHUNKS)):
-            load_x(i)
+        pieces = [(u, i) for u in range(4) for i in range(len(PIECES[u]))][2:]
+        for n, (u, i) in enumerate(pieces):
+            load_x(u, i)
+            if n < 4:
+                load_plane(2 * n)
+                load_plane(2 * n + 1)
+            if n == 4:
+                nc.sync.dma_start(bias[:], b)
         nc.sync.dma_start(w8[:].bitcast(I32), w8_words.rearrange("e a p n t -> p (e a) (n t)").bitcast(I32))
         nc.sync.dma_start(w4[:].bitcast(I32), w4_words.rearrange("e a p m -> p (e a) m").bitcast(I32))
-        nc.sync.dma_start(bias[:], b)
-        load_planes(4, w8_scales)
-        load_planes(0, w4_scales)
         nc.sync.dma_start(gates[:], gate)
         nc.sync.dma_start(resid[:], xr)
 
-        def cast(i):
-            a, c0, w, s = CHUNKS[i]
-            for engine_copy, lo, hi in ((scalar_copy, 0, s), (nc.vector.tensor_copy, s, w)):
-                if hi > lo:
-                    engine_copy(
-                        groups[i][:, lo:hi, :].rearrange("p (c i) j -> p c j i", i=4),
-                        raws[i][:, :, lo:hi].rearrange("p j (c i) -> p c j i", i=4),
-                    )
-
-        def scalar_copy(dst, src):
+        def scalar_cast(dst, src):
             nc.scalar.activation(dst, src, COPY)
 
-        def quantise(i):
-            a, c0, w, s = CHUNKS[i]
-            first = 4 if a == 0 else 0
+        def cast(u):
+            for i, (c0, w, s) in enumerate(PIECES[u]):
+                for engine_copy, lo, hi in ((scalar_cast, 0, s), (nc.vector.tensor_copy, s, w)):
+                    if hi > lo:
+                        engine_copy(
+                            pairs[u][:, c0 + lo : c0 + hi, :],
+                            raws[u][i][:, :, lo:hi].rearrange("p j w -> p w j"),
+                        )
+
+        def gather(dst, u, lo, hi):
+            window = pairs[u][:].rearrange("p t j -> p (t j)").bitcast(U32)
+            nc.vector.tensor_copy(dst, window.indirect(offsets[:, lo // 16 : hi // 16]))
+
+        def quantise(codes, scales, woven):
             nc.vector.quantize_mx(
-                out=words[a][:, c0 : c0 + w].bitcast(FP8X4),
-                scales=planes[first:P, c0 : c0 + w],
-                in_=groups[i][:].rearrange("p w j -> p (w j)"),
+                out=codes[:].bitcast(FP8X4),
+                scales=scales[:],
+                in_=woven[:].rearrange("p s h -> p (s h)").bitcast(BF16),
             )
-
-        def gather_words(a, lo, hi):
-            nc.vector.tensor_copy(slot_words[a][:, lo:hi], words[a][:].indirect(offsets[:, lo // 16 : hi // 16]))
-
-        def gather_planes(lo, hi):
-            nc.vector.tensor_copy(slot_planes[:, lo:hi], planes[:].indirect(offsets[:, lo // 16 : hi // 16]))
 
         def multiply(e):
             for h in range(C // 128):
-                cols = slice(e * C + h * 128, e * C + (h + 1) * 128)
-                acc = banks[e][:, h * 128 : (h + 1) * 128]
+                cols = slice(h * 128, (h + 1) * 128)
+                slots = slice(e * C + h * 128, e * C + (h + 1) * 128)
+                acc = banks[e][:, cols]
                 nc.tensor.matmul_mx(
                     out=acc,
                     lhsT=w8[:, e, :].bitcast(FP8X4),
                     lhsT_scale=w_planes[4:P, e, :],
-                    rhs=slot_words[0][:, cols].bitcast(FP8X4),
-                    rhs_scale=slot_planes[4:P, cols],
+                    rhs=codes0[:, slots].bitcast(FP8X4),
+                    rhs_scale=scales0[:, slots],
                     start=True,
                     stop=False,
                 )
@@ -132,30 +138,32 @@ def tile_moe_res_lin_relu_kernel(
                     out=acc,
                     lhsT=w4[:, e, :].bitcast(FP4X4),
                     lhsT_scale=w_planes[:, e, :],
-                    rhs=slot_words[1][:, cols].bitcast(FP8X4),
-                    rhs_scale=slot_planes[:, cols],
+                    rhs=codes1[e][:, cols].bitcast(FP8X4),
+                    rhs_scale=scales1[e][:, cols],
                     start=False,
                     stop=True,
                 )
-            nc.scalar.activation(ys[e // 2][:, (e % 2) * C : (e % 2 + 1) * C], banks[e][:], RELU, bias=bias[:, e : e + 1])
+            g = [k for k, (lo, hi) in enumerate(SCATTERS) if lo <= e < hi][0]
+            at = (e - SCATTERS[g][0]) * C
+            nc.scalar.activation(ys[g][:, at : at + C], banks[e][:], RELU, bias=bias[:, e : e + 1])
 
-        n = len(CHUNKS)
-        for i in range(n):
-            if i == 3:
-                quantise(2)
-                gather_words(0, 0, E * C)
-            cast(i)
-            if i >= 1 and i != 3:
-                quantise(i - 1)
-        quantise(n - 1)
-        for g in range(2):
-            gather_words(1, g * 512, (g + 1) * 512)
-            gather_planes(g * 512, (g + 1) * 512)
-            for e in (2 * g, 2 * g + 1):
-                multiply(e)
-        for g in range(2):
+        cast(0)
+        gather(woven0[:, :, 0], 0, 0, S)
+        cast(1)
+        gather(woven0[:, :, 1], 1, 0, S)
+        quantise(codes0, scales0, woven0)
+        cast(2)
+        gather(picked1[:, :, 0, :], 2, 0, S)
+        cast(3)
+        for e in range(E):
+            gather(picked1[:, e, 1, :], 3, e * C, (e + 1) * C)
+            nc.scalar.copy(woven1[e][:], picked1[:, e, :, :].rearrange("p h s -> p s h"))
+        for e in range(E):
+            quantise(codes1[e], scales1[e], woven1[e])
+            multiply(e)
+        for g, (lo, hi) in enumerate(SCATTERS):
             nc.vector.tensor_tensor(
-                routed[:].indirect(offsets[:, g * 32 : (g + 1) * 32]), ys[g][:], gates[:, g * 512 : (g + 1) * 512], MULT
+                routed[:].indirect(offsets[:, lo * C // 16 : hi * C // 16]), ys[g][:], gates[:, lo * C : hi * C], MULT
             )
 
         for i, (lo, hi) in enumerate(CUTS):

@@ -85,15 +85,15 @@ def tile_moe_res_lin_relu_kernel(
         load_x(0, 1)
         nc.sync.dma_start(offsets[:], offs)
         pieces = [(u, i) for u in range(4) for i in range(len(PIECES[u]))][2:]
-        for n, (u, i) in enumerate(pieces):
+        for u, i in pieces:
             load_x(u, i)
-            if n < 4:
-                load_plane(2 * n)
-                load_plane(2 * n + 1)
-            if n == 4:
-                nc.sync.dma_start(bias[:], b)
         nc.sync.dma_start(w8[:].bitcast(I32), w8_words.rearrange("e a p n t -> p (e a) (n t)").bitcast(I32))
+        for r in range(4):
+            load_plane(r)
         nc.sync.dma_start(w4[:].bitcast(I32), w4_words.rearrange("e a p m -> p (e a) m").bitcast(I32))
+        for r in range(4, 8):
+            load_plane(r)
+        nc.sync.dma_start(bias[:], b)
         nc.sync.dma_start(gates[:], gate)
         nc.sync.dma_start(resid[:], xr)
 

@@ -23,10 +23,11 @@ FLOPS = 2 * E * C * K * N
 
 PIECES = (
     ((0, 512, 512), (512, 768, 256), (1280, 256, 96)),
-    ((0, 512, 512), (512, 512, 512), (1024, 512, 224)),
+    ((0, 512, 512), (512, 512, 512), (1024, 512, 160)),
     ((0, 512, 512), (512, 512, 512), (1024, 512, 512)),
-    ((0, 512, 512), (512, 512, 512), (1024, 512, 320)),
+    ((0, 512, 512), (512, 512, 512), (1024, 512, 512)),
 )
+HALF = S // 2
 
 SCATTERS = ((0, 1), (1, 4))
 CUTS = ((0, 512), (512, 1024), (1024, 1536))
@@ -47,7 +48,8 @@ def tile_moe_res_lin_relu_kernel(
         ]
         pairs = [keep.tile([P, T, 2], BF16, name=f"pairs{u}", align_bytes=64) for u in range(4)]
         picked1 = keep.tile([P, E, 2, C], U32, name="picked1", align_bytes=64)
-        woven0 = keep.tile([P, S, 2], U32, name="woven0", align_bytes=64)
+        picked0 = [keep.tile([P, 2, HALF], U32, name=f"picked0_{g}", align_bytes=64) for g in range(2)]
+        woven0 = [keep.tile([P, HALF, 2], U32, name=f"woven0_{g}", align_bytes=64) for g in range(2)]
         woven1 = [keep.tile([P, C, 2], U32, name=f"woven1_{e}", align_bytes=64) for e in range(E)]
         codes0 = keep.tile([P, S], U32, name="codes0", align_bytes=64)
         scales0 = keep.tile([P, S], U8, name="scales0", align_bytes=64)
@@ -115,8 +117,8 @@ def tile_moe_res_lin_relu_kernel(
 
         def quantise(codes, scales, woven):
             nc.vector.quantize_mx(
-                out=codes[:].bitcast(FP8X4),
-                scales=scales[:],
+                out=codes.bitcast(FP8X4),
+                scales=scales,
                 in_=woven[:].rearrange("p s h -> p (s h)").bitcast(BF16),
             )
 
@@ -148,10 +150,16 @@ def tile_moe_res_lin_relu_kernel(
             nc.scalar.activation(ys[g][:, at : at + C], banks[e][:], RELU, bias=bias[:, e : e + 1])
 
         cast(0)
-        gather(woven0[:, :, 0], 0, 0, S)
+        for g in range(2):
+            gather(picked0[g][:, 0, :], 0, g * HALF, (g + 1) * HALF)
         cast(1)
-        gather(woven0[:, :, 1], 1, 0, S)
-        quantise(codes0, scales0, woven0)
+        for g in range(2):
+            gather(picked0[g][:, 1, :], 1, g * HALF, (g + 1) * HALF)
+        for g in range(2):
+            nc.vector.tensor_copy(woven0[g][:].bitcast(I32), picked0[g][:].bitcast(I32).rearrange("p h s -> p s h"))
+        for g in range(2):
+            half = slice(g * HALF, (g + 1) * HALF)
+            quantise(codes0[:, half], scales0[:, half], woven0[g])
         cast(2)
         gather(picked1[:, :, 0, :], 2, 0, S)
         cast(3)
@@ -159,7 +167,7 @@ def tile_moe_res_lin_relu_kernel(
             gather(picked1[:, e, 1, :], 3, e * C, (e + 1) * C)
             nc.scalar.copy(woven1[e][:], picked1[:, e, :, :].rearrange("p h s -> p s h"))
         for e in range(E):
-            quantise(codes1[e], scales1[e], woven1[e])
+            quantise(codes1[e][:], scales1[e][:], woven1[e])
             multiply(e)
         for g, (lo, hi) in enumerate(SCATTERS):
             nc.vector.tensor_tensor(

@@ -23,9 +23,9 @@ FLOPS = 2 * E * C * K * N
 
 PIECES = (
     ((0, 512, 512), (512, 768, 256), (1280, 256, 96)),
-    ((0, 512, 512), (512, 512, 512), (1024, 512, 160)),
-    ((0, 512, 512), (512, 512, 512), (1024, 512, 512)),
-    ((0, 512, 512), (512, 512, 512), (1024, 512, 512)),
+    ((0, 512, 512), (512, 768, 256), (1280, 256, 128)),
+    ((0, 384, 384), (384, 384, 384), (768, 384, 384), (1152, 384, 384)),
+    ((0, 384, 384), (384, 384, 384), (768, 384, 384), (1152, 384, 384)),
 )
 HALF = S // 2
 
@@ -47,7 +47,7 @@ def tile_moe_res_lin_relu_kernel(
             for u in range(4)
         ]
         pairs = [keep.tile([P, T, 2], BF16, name=f"pairs{u}", align_bytes=64) for u in range(4)]
-        picked1 = keep.tile([P, E, 2, C], U32, name="picked1", align_bytes=64)
+        picked1 = keep.tile([P, 2, S], U32, name="picked1", align_bytes=64)
         picked0 = [keep.tile([P, 2, HALF], U32, name=f"picked0_{g}", align_bytes=64) for g in range(2)]
         woven0 = [keep.tile([P, HALF, 2], U32, name=f"woven0_{g}", align_bytes=64) for g in range(2)]
         woven1 = [keep.tile([P, C, 2], U32, name=f"woven1_{e}", align_bytes=64) for e in range(E)]
@@ -64,7 +64,7 @@ def tile_moe_res_lin_relu_kernel(
         ys = [keep.tile([P, (hi - lo) * C], F32, name=f"y{g}") for g, (lo, hi) in enumerate(SCATTERS)]
         routed = keep.tile([P, T], F32, name="routed")
         sums = [keep.tile([P, hi - lo], F32, name=f"sum{i}") for i, (lo, hi) in enumerate(CUTS)]
-        banks = [psum.tile([P, C], F32, name=f"bank{e}") for e in range(E)]
+        banks = [psum.tile([P, 128], F32, name=f"bank{n}") for n in range(S // 128)]
 
         nc.gpsimd.memset(w_planes[:].rearrange("p e n -> p (e n)").bitcast(I32), 0)
         nc.vector.memset(routed[:], 0.0)
@@ -99,6 +99,9 @@ def tile_moe_res_lin_relu_kernel(
         nc.sync.dma_start(gates[:], gate)
         nc.sync.dma_start(resid[:], xr)
 
+        def by_fours(dst, src):
+            return dst.rearrange("p (c i) j -> p c j i", i=4), src.rearrange("p j (c i) -> p c j i", i=4)
+
         def scalar_cast(dst, src):
             nc.scalar.activation(dst, src, COPY)
 
@@ -106,10 +109,7 @@ def tile_moe_res_lin_relu_kernel(
             for i, (c0, w, s) in enumerate(PIECES[u]):
                 for engine_copy, lo, hi in ((scalar_cast, 0, s), (nc.vector.tensor_copy, s, w)):
                     if hi > lo:
-                        engine_copy(
-                            pairs[u][:, c0 + lo : c0 + hi, :],
-                            raws[u][i][:, :, lo:hi].rearrange("p j w -> p w j"),
-                        )
+                        engine_copy(*by_fours(pairs[u][:, c0 + lo : c0 + hi, :], raws[u][i][:, :, lo:hi]))
 
         def gather(dst, u, lo, hi):
             window = pairs[u][:].rearrange("p t j -> p (t j)").bitcast(U32)
@@ -122,13 +122,11 @@ def tile_moe_res_lin_relu_kernel(
                 in_=woven[:].rearrange("p s h -> p (s h)").bitcast(BF16),
             )
 
-        def multiply(e):
-            for h in range(C // 128):
-                cols = slice(h * 128, (h + 1) * 128)
-                slots = slice(e * C + h * 128, e * C + (h + 1) * 128)
-                acc = banks[e][:, cols]
+        def open_sums(e):
+            for n in (2 * e, 2 * e + 1):
+                slots = slice(n * 128, (n + 1) * 128)
                 nc.tensor.matmul_mx(
-                    out=acc,
+                    out=banks[n][:],
                     lhsT=w8[:, e, :].bitcast(FP8X4),
                     lhsT_scale=w_planes[4:P, e, :],
                     rhs=codes0[:, slots].bitcast(FP8X4),
@@ -136,8 +134,13 @@ def tile_moe_res_lin_relu_kernel(
                     start=True,
                     stop=False,
                 )
+
+        def close_sums(e):
+            g = [k for k, (lo, hi) in enumerate(SCATTERS) if lo <= e < hi][0]
+            for h in range(2):
+                cols = slice(h * 128, (h + 1) * 128)
                 nc.tensor.matmul_mx(
-                    out=acc,
+                    out=banks[2 * e + h][:],
                     lhsT=w4[:, e, :].bitcast(FP4X4),
                     lhsT_scale=w_planes[:, e, :],
                     rhs=codes1[e][:, cols].bitcast(FP8X4),
@@ -145,9 +148,8 @@ def tile_moe_res_lin_relu_kernel(
                     start=False,
                     stop=True,
                 )
-            g = [k for k, (lo, hi) in enumerate(SCATTERS) if lo <= e < hi][0]
-            at = (e - SCATTERS[g][0]) * C
-            nc.scalar.activation(ys[g][:, at : at + C], banks[e][:], RELU, bias=bias[:, e : e + 1])
+                at = (e - SCATTERS[g][0]) * C + h * 128
+                nc.scalar.activation(ys[g][:, at : at + 128], banks[2 * e + h][:], RELU, bias=bias[:, e : e + 1])
 
         cast(0)
         for g in range(2):
@@ -156,19 +158,20 @@ def tile_moe_res_lin_relu_kernel(
         for g in range(2):
             gather(picked0[g][:, 1, :], 1, g * HALF, (g + 1) * HALF)
         for g in range(2):
-            nc.vector.tensor_copy(woven0[g][:].bitcast(I32), picked0[g][:].bitcast(I32).rearrange("p h s -> p s h"))
+            nc.vector.tensor_copy(*by_fours(woven0[g][:].bitcast(I32), picked0[g][:].bitcast(I32)))
         for g in range(2):
             half = slice(g * HALF, (g + 1) * HALF)
             quantise(codes0[:, half], scales0[:, half], woven0[g])
         cast(2)
-        gather(picked1[:, :, 0, :], 2, 0, S)
+        gather(picked1[:, 0, :], 2, 0, S)
         cast(3)
         for e in range(E):
-            gather(picked1[:, e, 1, :], 3, e * C, (e + 1) * C)
-            nc.scalar.copy(woven1[e][:], picked1[:, e, :, :].rearrange("p h s -> p s h"))
+            gather(picked1[:, 1, e * C : (e + 1) * C], 3, e * C, (e + 1) * C)
+            nc.scalar.copy(*by_fours(woven1[e][:], picked1[:, :, e * C : (e + 1) * C]))
         for e in range(E):
             quantise(codes1[e][:], scales1[e][:], woven1[e])
-            multiply(e)
+            open_sums(e)
+            close_sums(e)
         for g, (lo, hi) in enumerate(SCATTERS):
             nc.vector.tensor_tensor(
                 routed[:].indirect(offsets[:, lo * C // 16 : hi * C // 16]), ys[g][:], gates[:, lo * C : hi * C], MULT

@@ -22,10 +22,10 @@ PASS = 512
 FLOPS = 2 * E * C * K * N
 
 PIECES = (
-    ((0, 512, 512), (512, 768, 256), (1280, 256, 96)),
+    ((0, 1024, 448), (1024, 512, 160)),
     ((0, 512, 512), (512, 768, 256), (1280, 256, 128)),
-    ((0, 384, 384), (384, 384, 384), (768, 384, 384), (1152, 384, 384)),
-    ((0, 384, 384), (384, 384, 384), (768, 384, 384), (1152, 384, 384)),
+    ((0, 512, 512), (512, 512, 512), (1024, 512, 512)),
+    ((0, 448, 448), (448, 384, 384), (832, 384, 384), (1216, 320, 320)),
 )
 HALF = S // 2
 

@@ -22,8 +22,8 @@ PASS = 512
 FLOPS = 2 * E * C * K * N
 
 PIECES = (
-    ((0, 1024, 448), (1024, 512, 160)),
-    ((0, 512, 512), (512, 768, 256), (1280, 256, 128)),
+    ((0, 1536, 544),),
+    ((0, 512, 512), (512, 512, 512), (1024, 512, 160)),
     ((0, 512, 512), (512, 512, 512), (1024, 512, 512)),
     ((0, 448, 448), (448, 384, 384), (832, 384, 384), (1216, 320, 320)),
 )
@@ -84,9 +84,8 @@ def tile_moe_res_lin_relu_kernel(
             )
 
         load_x(0, 0)
-        load_x(0, 1)
         nc.sync.dma_start(offsets[:], offs)
-        pieces = [(u, i) for u in range(4) for i in range(len(PIECES[u]))][2:]
+        pieces = [(u, i) for u in range(4) for i in range(len(PIECES[u]))][1:]
         for u, i in pieces:
             load_x(u, i)
         nc.sync.dma_start(w8[:].bitcast(I32), w8_words.rearrange("e a p n t -> p (e a) (n t)").bitcast(I32))

@@ -99,7 +99,7 @@ def tile_moe_res_lin_relu_kernel(
         nc.sync.dma_start(resid[:], xr)
 
         def by_fours(dst, src):
-            return dst.rearrange("p (c i) j -> p c j i", i=4), src.rearrange("p j (c i) -> p c j i", i=4)
+            return dst, src.rearrange("p j c -> p c j")
 
         def scalar_cast(dst, src):
             nc.scalar.activation(dst, src, COPY)

@@ -22,15 +22,15 @@ PASS = 512
 FLOPS = 2 * E * C * K * N
 
 PIECES = (
-    ((0, 1536, 544),),
-    ((0, 512, 512), (512, 512, 512), (1024, 512, 160)),
-    ((0, 512, 512), (512, 512, 512), (1024, 512, 512)),
-    ((0, 448, 448), (448, 384, 384), (832, 384, 384), (1216, 320, 320)),
+    ((0, 1536, 544, 0),),
+    ((0, 512, 512, 0), (512, 512, 512, 0), (1024, 512, 160, 0),),
+    ((0, 512, 384, 128), (512, 512, 512, 0), (1024, 512, 512, 0),),
+    ((0, 448, 448, 0), (448, 384, 384, 0), (832, 384, 384, 0), (1216, 320, 224, 96),),
 )
 HALF = S // 2
 
 SCATTERS = ((0, 1), (1, 4))
-CUTS = ((0, 512), (512, 1024), (1024, 1536))
+CUTS = ((0, 256), (256, 608), (608, 1024), (1024, 1536))
 
 
 def tile_moe_res_lin_relu_kernel(
@@ -43,7 +43,7 @@ def tile_moe_res_lin_relu_kernel(
 
         offsets = keep.tile([P, S // 16], U16, name="offsets")
         raws = [
-            [keep.tile([P, 2, w], F32, name=f"raw{u}_{i}", align_bytes=64) for i, (c0, w, s) in enumerate(PIECES[u])]
+            [keep.tile([P, 2, w], F32, name=f"raw{u}_{i}", align_bytes=64) for i, (c0, w, s, g) in enumerate(PIECES[u])]
             for u in range(4)
         ]
         pairs = [keep.tile([P, T, 2], BF16, name=f"pairs{u}", align_bytes=64) for u in range(4)]
@@ -70,7 +70,7 @@ def tile_moe_res_lin_relu_kernel(
         nc.vector.memset(routed[:], 0.0)
 
         def load_x(u, i):
-            c0, w, s = PIECES[u][i]
+            c0, w, s, g = PIECES[u][i]
             a, h = divmod(u, 2)
             src = xT[PASS * a : PASS * (a + 1), c0 : c0 + w].rearrange("(p j) w -> p j w", j=4)
             nc.sync.dma_start(raws[u][i][:], src[:, 2 * h : 2 * h + 2, :])
@@ -105,8 +105,8 @@ def tile_moe_res_lin_relu_kernel(
             nc.scalar.activation(dst, src, COPY)
 
         def cast(u):
-            for i, (c0, w, s) in enumerate(PIECES[u]):
-                for engine_copy, lo, hi in ((scalar_cast, 0, s), (nc.vector.tensor_copy, s, w)):
+            for i, (c0, w, s, g) in enumerate(PIECES[u]):
+                for engine_copy, lo, hi in ((scalar_cast, 0, s), (nc.gpsimd.tensor_copy, s, s + g), (nc.vector.tensor_copy, s + g, w)):
                     if hi > lo:
                         engine_copy(*by_fours(pairs[u][:, c0 + lo : c0 + hi, :], raws[u][i][:, :, lo:hi]))
 

@@ -23,11 +23,14 @@ FLOPS = 2 * E * C * K * N
 
 PIECES = (
     ((0, 1536, 544, 0),),
-    ((0, 512, 512, 0), (512, 512, 512, 0), (1024, 512, 160, 0),),
-    ((0, 512, 384, 128), (512, 512, 512, 0), (1024, 512, 512, 0),),
-    ((0, 448, 448, 0), (448, 384, 384, 0), (832, 384, 384, 0), (1216, 320, 224, 96),),
+    ((0, 704, 448, 256), (704, 576, 368, 208), (1280, 256, 176, 80),),
+    ((0, 512, 512, 0), (512, 512, 512, 0), (1024, 512, 512, 0),),
+    ((0, 640, 400, 240), (640, 576, 360, 216), (1216, 320, 208, 112),),
 )
 HALF = S // 2
+GATHERS1 = ((0, 256), (256, 512), (512, 1024))
+WEAVES_GPSIMD = ((0, 256), (256, 384))
+WEAVES_VECTOR = ((384, 512), (512, 1024))
 
 SCATTERS = ((0, 1), (1, 4))
 CUTS = ((0, 256), (256, 608), (608, 1024), (1024, 1536))
@@ -48,8 +51,8 @@ def tile_moe_res_lin_relu_kernel(
         ]
         pairs = [keep.tile([P, T, 2], BF16, name=f"pairs{u}", align_bytes=64) for u in range(4)]
         picked1 = keep.tile([P, 2, S], U32, name="picked1", align_bytes=64)
-        picked0 = [keep.tile([P, 2, HALF], U32, name=f"picked0_{g}", align_bytes=64) for g in range(2)]
-        woven0 = [keep.tile([P, HALF, 2], U32, name=f"woven0_{g}", align_bytes=64) for g in range(2)]
+        picked0 = keep.tile([P, 2, S], U32, name="picked0", align_bytes=64)
+        woven0 = keep.tile([P, S, 2], U32, name="woven0", align_bytes=64)
         woven1 = [keep.tile([P, C, 2], U32, name=f"woven1_{e}", align_bytes=64) for e in range(E)]
         codes0 = keep.tile([P, S], U32, name="codes0", align_bytes=64)
         scales0 = keep.tile([P, S], U8, name="scales0", align_bytes=64)
@@ -118,7 +121,7 @@ def tile_moe_res_lin_relu_kernel(
             nc.vector.quantize_mx(
                 out=codes.bitcast(FP8X4),
                 scales=scales,
-                in_=woven[:].rearrange("p s h -> p (s h)").bitcast(BF16),
+                in_=woven.rearrange("p s h -> p (s h)").bitcast(BF16),
             )
 
         def open_sums(e):
@@ -151,16 +154,16 @@ def tile_moe_res_lin_relu_kernel(
                 nc.scalar.activation(ys[g][:, at : at + 128], banks[2 * e + h][:], RELU, bias=bias[:, e : e + 1])
 
         cast(0)
-        for g in range(2):
-            gather(picked0[g][:, 0, :], 0, g * HALF, (g + 1) * HALF)
+        gather(picked0[:, 0, :], 0, 0, S)
         cast(1)
-        for g in range(2):
-            gather(picked0[g][:, 1, :], 1, g * HALF, (g + 1) * HALF)
-        for g in range(2):
-            nc.vector.tensor_copy(*by_fours(woven0[g][:].bitcast(I32), picked0[g][:].bitcast(I32)))
+        for lo, hi in GATHERS1:
+            gather(picked0[:, 1, lo:hi], 1, lo, hi)
+        for engine, cuts in ((nc.gpsimd, WEAVES_GPSIMD), (nc.vector, WEAVES_VECTOR)):
+            for lo, hi in cuts:
+                engine.tensor_copy(*by_fours(woven0[:, lo:hi, :].bitcast(I32), picked0[:, :, lo:hi].bitcast(I32)))
         for g in range(2):
             half = slice(g * HALF, (g + 1) * HALF)
-            quantise(codes0[:, half], scales0[:, half], woven0[g])
+            quantise(codes0[:, half], scales0[:, half], woven0[:, half, :])
         cast(2)
         gather(picked1[:, 0, :], 2, 0, S)
         cast(3)
@@ -168,7 +171,7 @@ def tile_moe_res_lin_relu_kernel(
             gather(picked1[:, 1, e * C : (e + 1) * C], 3, e * C, (e + 1) * C)
             nc.scalar.copy(*by_fours(woven1[e][:], picked1[:, :, e * C : (e + 1) * C]))
         for e in range(E):
-            quantise(codes1[e][:], scales1[e][:], woven1[e])
+            quantise(codes1[e][:], scales1[e][:], woven1[e][:])
             open_sums(e)
             close_sums(e)
         for g, (lo, hi) in enumerate(SCATTERS):

@@ -23,14 +23,14 @@ FLOPS = 2 * E * C * K * N
 
 PIECES = (
     ((0, 1536, 544, 0),),
-    ((0, 704, 448, 256), (704, 576, 368, 208), (1280, 256, 176, 80),),
-    ((0, 512, 512, 0), (512, 512, 512, 0), (1024, 512, 512, 0),),
-    ((0, 640, 400, 240), (640, 576, 360, 216), (1216, 320, 208, 112),),
+    ((0, 960, 608, 352), (960, 576, 352, 0),),
+    ((0, 800, 800, 0), (800, 736, 736, 0),),
+    ((0, 800, 512, 288), (800, 480, 320, 160), (1280, 256, 192, 64),),
 )
 HALF = S // 2
-GATHERS1 = ((0, 256), (256, 512), (512, 1024))
-WEAVES_GPSIMD = ((0, 256), (256, 384))
-WEAVES_VECTOR = ((384, 512), (512, 1024))
+GATHERS1 = ((0, 192), (192, 512), (512, 1024))
+WEAVES_GPSIMD = ((0, 192), (192, 512))
+WEAVES_VECTOR = ((512, 1024),)
 
 SCATTERS = ((0, 1), (1, 4))
 CUTS = ((0, 256), (256, 608), (608, 1024), (1024, 1536))

@@ -22,10 +22,10 @@ PASS = 512
 FLOPS = 2 * E * C * K * N
 
 PIECES = (
-    ((0, 1536, 544, 0),),
-    ((0, 960, 608, 352), (960, 576, 352, 0),),
-    ((0, 800, 800, 0), (800, 736, 736, 0),),
-    ((0, 800, 512, 288), (800, 480, 320, 160), (1280, 256, 192, 64),),
+    ((0, 1536, 560, 0),),
+    ((0, 1024, 640, 384), (1024, 512, 288, 0),),
+    ((0, 768, 768, 0), (768, 768, 768, 0),),
+    ((0, 768, 496, 272), (768, 512, 336, 176), (1280, 256, 192, 64),),
 )
 HALF = S // 2
 GATHERS1 = ((0, 192), (192, 512), (512, 1024))

@@ -19,21 +19,27 @@ P = 128
 K, T, E, C, N = 1024, 1536, 4, 256, 128
 S = E * C
 PASS = 512
+GROUP = 128
+LIST = 16
 FLOPS = 2 * E * C * K * N
 
 PIECES = (
-    ((0, 1536, 560, 0),),
-    ((0, 1024, 640, 384), (1024, 512, 288, 0),),
-    ((0, 768, 768, 0), (768, 768, 768, 0),),
-    ((0, 768, 496, 272), (768, 512, 336, 176), (1280, 256, 192, 64),),
+    ((1536, "vector"),),
+    ((1024, "gpsimd"), (512, "vector")),
+    ((768, "none"), (768, "none")),
+    ((768, "gpsimd"), (512, "gpsimd"), (256, "gpsimd")),
 )
-HALF = S // 2
-GATHERS1 = ((0, 192), (192, 512), (512, 1024))
-WEAVES_GPSIMD = ((0, 192), (192, 512))
-WEAVES_VECTOR = ((512, 1024),)
+SCALAR_SHARE = {"vector": 9, "gpsimd": 16, "none": 24}
+SHARE_STEP = 16
 
-SCATTERS = ((0, 1), (1, 4))
-CUTS = ((0, 256), (256, 608), (608, 1024), (1024, 1536))
+HALF = S // 2
+GPSIMD_WEAVES = ((0, 192), (192, HALF))
+VECTOR_WEAVE = (HALF, S)
+
+SCATTERS = ((0, 1), (1, E))
+CUTS = ((0, 256), (256, 608), (608, 1024), (1024, T))
+
+FIRST8, FIRST4 = 4, 0
 
 
 def tile_moe_res_lin_relu_kernel(
@@ -44,9 +50,9 @@ def tile_moe_res_lin_relu_kernel(
         keep = ctx.enter_context(tc.tile_pool(name="keep", bufs=1))
         psum = ctx.enter_context(tc.psum_pool(name="psum", bufs=1))
 
-        offsets = keep.tile([P, S // 16], U16, name="offsets")
+        offsets = keep.tile([P, S // LIST], U16, name="offsets")
         raws = [
-            [keep.tile([P, 2, w], F32, name=f"raw{u}_{i}", align_bytes=64) for i, (c0, w, s, g) in enumerate(PIECES[u])]
+            [keep.tile([P, 2, tokens], F32, name=f"raw{u}_{i}", align_bytes=64) for i, (tokens, helper) in enumerate(PIECES[u])]
             for u in range(4)
         ]
         pairs = [keep.tile([P, T, 2], BF16, name=f"pairs{u}", align_bytes=64) for u in range(4)]
@@ -60,62 +66,65 @@ def tile_moe_res_lin_relu_kernel(
         scales1 = [keep.tile([P, C], U8, name=f"scales1_{e}", align_bytes=64) for e in range(E)]
         w8 = keep.tile([P, E, 4 * N], U8, name="w8", align_bytes=64)
         w4 = keep.tile([P, E, 2 * N], U8, name="w4", align_bytes=64)
-        w_planes = keep.tile([P, E, N], U8, name="w_planes", align_bytes=64)
+        w_scales = keep.tile([P, E, N], U8, name="w_scales", align_bytes=64)
         bias = keep.tile([P, E], F32, name="bias")
         gates = keep.tile([P, S], F32, name="gates")
         resid = keep.tile([P, T], F32, name="resid")
         ys = [keep.tile([P, (hi - lo) * C], F32, name=f"y{g}") for g, (lo, hi) in enumerate(SCATTERS)]
         routed = keep.tile([P, T], F32, name="routed")
         sums = [keep.tile([P, hi - lo], F32, name=f"sum{i}") for i, (lo, hi) in enumerate(CUTS)]
-        banks = [psum.tile([P, 128], F32, name=f"bank{n}") for n in range(S // 128)]
+        banks = [psum.tile([P, GROUP], F32, name=f"bank{n}") for n in range(S // GROUP)]
 
-        nc.gpsimd.memset(w_planes[:].rearrange("p e n -> p (e n)").bitcast(I32), 0)
+        nc.gpsimd.memset(w_scales[:].rearrange("p e n -> p (e n)").bitcast(I32), 0)
         nc.vector.memset(routed[:], 0.0)
 
-        def load_x(u, i):
-            c0, w, s, g = PIECES[u][i]
-            a, h = divmod(u, 2)
-            src = xT[PASS * a : PASS * (a + 1), c0 : c0 + w].rearrange("(p j) w -> p j w", j=4)
-            nc.sync.dma_start(raws[u][i][:], src[:, 2 * h : 2 * h + 2, :])
+        def first_token(u, i):
+            return sum(tokens for tokens, helper in PIECES[u][:i])
 
-        def load_plane(r):
-            first, scales = ((4, w8_scales), (0, w4_scales))[r // 4]
-            q = r % 4
-            nc.sync.dma_start(
-                w_planes[32 * q + first : 32 * q + first + 4, :, :].bitcast(I32),
-                scales[:, 0, 4 * q : 4 * q + 4, :].rearrange("e q n -> q e n").bitcast(I32),
-            )
+        def load_x(u, i):
+            a, h = divmod(u, 2)
+            start = first_token(u, i)
+            rows = xT[PASS * a : PASS * (a + 1), start : start + PIECES[u][i][0]].rearrange("(p t) w -> p t w", t=4)
+            nc.sync.dma_start(raws[u][i][:], rows[:, 2 * h : 2 * h + 2, :])
+
+        def load_scale_rows(scales, first):
+            for quadrant in range(4):
+                nc.sync.dma_start(
+                    w_scales[32 * quadrant + first : 32 * quadrant + first + 4, :, :].bitcast(I32),
+                    scales[:, 0, 4 * quadrant : 4 * quadrant + 4, :].rearrange("e q n -> q e n").bitcast(I32),
+                )
 
         load_x(0, 0)
         nc.sync.dma_start(offsets[:], offs)
-        pieces = [(u, i) for u in range(4) for i in range(len(PIECES[u]))][1:]
-        for u, i in pieces:
-            load_x(u, i)
+        for u in range(1, 4):
+            for i in range(len(PIECES[u])):
+                load_x(u, i)
         nc.sync.dma_start(w8[:].bitcast(I32), w8_words.rearrange("e a p n t -> p (e a) (n t)").bitcast(I32))
-        for r in range(4):
-            load_plane(r)
+        load_scale_rows(w8_scales, FIRST8)
         nc.sync.dma_start(w4[:].bitcast(I32), w4_words.rearrange("e a p m -> p (e a) m").bitcast(I32))
-        for r in range(4, 8):
-            load_plane(r)
+        load_scale_rows(w4_scales, FIRST4)
         nc.sync.dma_start(bias[:], b)
         nc.sync.dma_start(gates[:], gate)
         nc.sync.dma_start(resid[:], xr)
 
-        def by_fours(dst, src):
-            return dst, src.rearrange("p j c -> p c j")
+        def side_by_side(two_rows):
+            return two_rows.rearrange("p j c -> p c j")
 
-        def scalar_cast(dst, src):
-            nc.scalar.activation(dst, src, COPY)
+        def round_pair(u):
+            for i, (tokens, helper) in enumerate(PIECES[u]):
+                start = first_token(u, i)
+                share = round(tokens * SCALAR_SHARE[helper] / 24 / SHARE_STEP) * SHARE_STEP
+                nc.scalar.activation(pairs[u][:, start : start + share, :], side_by_side(raws[u][i][:, :, :share]), COPY)
+                if helper != "none":
+                    engine = nc.vector if helper == "vector" else nc.gpsimd
+                    engine.tensor_copy(pairs[u][:, start + share : start + tokens, :], side_by_side(raws[u][i][:, :, share:]))
 
-        def cast(u):
-            for i, (c0, w, s, g) in enumerate(PIECES[u]):
-                for engine_copy, lo, hi in ((scalar_cast, 0, s), (nc.gpsimd.tensor_copy, s, s + g), (nc.vector.tensor_copy, s + g, w)):
-                    if hi > lo:
-                        engine_copy(*by_fours(pairs[u][:, c0 + lo : c0 + hi, :], raws[u][i][:, :, lo:hi]))
-
-        def gather(dst, u, lo, hi):
+        def gather(picked, u, lo, hi):
             window = pairs[u][:].rearrange("p t j -> p (t j)").bitcast(U32)
-            nc.vector.tensor_copy(dst, window.indirect(offsets[:, lo // 16 : hi // 16]))
+            nc.vector.tensor_copy(picked[:, u % 2, lo:hi], window.indirect(offsets[:, lo // LIST : hi // LIST]))
+
+        def weave0(engine, lo, hi):
+            engine.tensor_copy(woven0[:, lo:hi, :].bitcast(I32), side_by_side(picked0[:, :, lo:hi].bitcast(I32)))
 
         def quantise(codes, scales, woven):
             nc.vector.quantize_mx(
@@ -126,11 +135,11 @@ def tile_moe_res_lin_relu_kernel(
 
         def open_sums(e):
             for n in (2 * e, 2 * e + 1):
-                slots = slice(n * 128, (n + 1) * 128)
+                slots = slice(n * GROUP, (n + 1) * GROUP)
                 nc.tensor.matmul_mx(
                     out=banks[n][:],
                     lhsT=w8[:, e, :].bitcast(FP8X4),
-                    lhsT_scale=w_planes[4:P, e, :],
+                    lhsT_scale=w_scales[FIRST8:P, e, :],
                     rhs=codes0[:, slots].bitcast(FP8X4),
                     rhs_scale=scales0[:, slots],
                     start=True,
@@ -138,48 +147,46 @@ def tile_moe_res_lin_relu_kernel(
                 )
 
         def close_sums(e):
-            g = [k for k, (lo, hi) in enumerate(SCATTERS) if lo <= e < hi][0]
-            for h in range(2):
-                cols = slice(h * 128, (h + 1) * 128)
+            g = 0 if e < SCATTERS[0][1] else 1
+            for half in range(2):
+                places = slice(half * GROUP, (half + 1) * GROUP)
                 nc.tensor.matmul_mx(
-                    out=banks[2 * e + h][:],
+                    out=banks[2 * e + half][:],
                     lhsT=w4[:, e, :].bitcast(FP4X4),
-                    lhsT_scale=w_planes[:, e, :],
-                    rhs=codes1[e][:, cols].bitcast(FP8X4),
-                    rhs_scale=scales1[e][:, cols],
+                    lhsT_scale=w_scales[FIRST4:P, e, :],
+                    rhs=codes1[e][:, places].bitcast(FP8X4),
+                    rhs_scale=scales1[e][:, places],
                     start=False,
                     stop=True,
                 )
-                at = (e - SCATTERS[g][0]) * C + h * 128
-                nc.scalar.activation(ys[g][:, at : at + 128], banks[2 * e + h][:], RELU, bias=bias[:, e : e + 1])
+                at = (e - SCATTERS[g][0]) * C + half * GROUP
+                nc.scalar.activation(ys[g][:, at : at + GROUP], banks[2 * e + half][:], RELU, bias=bias[:, e : e + 1])
 
-        cast(0)
-        gather(picked0[:, 0, :], 0, 0, S)
-        cast(1)
-        for lo, hi in GATHERS1:
-            gather(picked0[:, 1, lo:hi], 1, lo, hi)
-        for engine, cuts in ((nc.gpsimd, WEAVES_GPSIMD), (nc.vector, WEAVES_VECTOR)):
-            for lo, hi in cuts:
-                engine.tensor_copy(*by_fours(woven0[:, lo:hi, :].bitcast(I32), picked0[:, :, lo:hi].bitcast(I32)))
-        for g in range(2):
-            half = slice(g * HALF, (g + 1) * HALF)
-            quantise(codes0[:, half], scales0[:, half], woven0[:, half, :])
-        cast(2)
-        gather(picked1[:, 0, :], 2, 0, S)
-        cast(3)
+        round_pair(0)
+        gather(picked0, 0, 0, S)
+        round_pair(1)
+        for lo, hi in GPSIMD_WEAVES + (VECTOR_WEAVE,):
+            gather(picked0, 1, lo, hi)
+        for lo, hi in GPSIMD_WEAVES:
+            weave0(nc.gpsimd, lo, hi)
+        weave0(nc.vector, *VECTOR_WEAVE)
+        for lo in (0, HALF):
+            quantise(codes0[:, lo : lo + HALF], scales0[:, lo : lo + HALF], woven0[:, lo : lo + HALF, :])
+
+        round_pair(2)
+        gather(picked1, 2, 0, S)
+        round_pair(3)
         for e in range(E):
-            gather(picked1[:, 1, e * C : (e + 1) * C], 3, e * C, (e + 1) * C)
-            nc.scalar.copy(*by_fours(woven1[e][:], picked1[:, :, e * C : (e + 1) * C]))
+            gather(picked1, 3, e * C, (e + 1) * C)
+            nc.scalar.copy(woven1[e][:], side_by_side(picked1[:, :, e * C : (e + 1) * C]))
         for e in range(E):
             quantise(codes1[e][:], scales1[e][:], woven1[e][:])
             open_sums(e)
             close_sums(e)
-        for g, (lo, hi) in enumerate(SCATTERS):
-            nc.vector.tensor_tensor(
-                routed[:].indirect(offsets[:, lo * C // 16 : hi * C // 16]), ys[g][:], gates[:, lo * C : hi * C], MULT
-            )
 
+        for g, (lo, hi) in enumerate(SCATTERS):
+            window = routed[:].indirect(offsets[:, lo * C // LIST : hi * C // LIST])
+            nc.vector.tensor_tensor(window, ys[g][:], gates[:, lo * C : hi * C], MULT)
         for i, (lo, hi) in enumerate(CUTS):
-            cols = slice(lo, hi)
-            nc.vector.tensor_tensor(sums[i][:], routed[:, cols], resid[:, cols], ADD)
-            nc.sync.dma_start(out[:, cols], sums[i][:])
+            nc.vector.tensor_tensor(sums[i][:], routed[:, lo:hi], resid[:, lo:hi], ADD)
+            nc.sync.dma_start(out[:, lo:hi], sums[i][:])

@@ -33,11 +33,14 @@ SCALAR_SHARE = {"vector": 9, "gpsimd": 16, "none": 24}
 SHARE_STEP = 16
 
 HALF = S // 2
-GPSIMD_WEAVES = ((0, 192), (192, HALF))
-VECTOR_WEAVE = (HALF, S)
+GPSIMD_WEAVES = ((0, 192), (192, 384))
+VECTOR_WEAVE = (384, S)
 
 SCATTERS = ((0, 1), (1, E))
-CUTS = ((0, 256), (256, 608), (608, 1024), (1024, T))
+FIRST_CUT, LATER_CUTS = 256, 4
+CUTS = ((0, FIRST_CUT),) + tuple(
+    (FIRST_CUT + i * (T - FIRST_CUT) // LATER_CUTS, FIRST_CUT + (i + 1) * (T - FIRST_CUT) // LATER_CUTS) for i in range(LATER_CUTS)
+)
 
 FIRST8, FIRST4 = 4, 0
 

@@ -24,8 +24,8 @@ LIST = 16
 FLOPS = 2 * E * C * K * N
 
 PIECES = (
-    ((1536, "vector"),),
-    ((1024, "gpsimd"), (512, "vector")),
+    ((768, "vector"), (768, "vector")),
+    ((896, "gpsimd"), (640, "vector")),
     ((768, "none"), (768, "none")),
     ((768, "gpsimd"), (512, "gpsimd"), (256, "gpsimd")),
 )
@@ -33,8 +33,8 @@ SCALAR_SHARE = {"vector": 9, "gpsimd": 16, "none": 24}
 SHARE_STEP = 16
 
 HALF = S // 2
-GPSIMD_WEAVES = ((0, 192), (192, 384))
-VECTOR_WEAVE = (384, S)
+GPSIMD_WEAVES = ((0, 192), (192, HALF))
+VECTOR_WEAVE = (HALF, S)
 
 SCATTERS = ((0, 1), (1, E))
 FIRST_CUT, LATER_CUTS = 256, 4
@@ -56,8 +56,10 @@ def tile_moe_res_lin_relu_kernel(
         offsets = keep.tile([P, S // LIST], U16, name="offsets")
         raws = [
             [keep.tile([P, 2, tokens], F32, name=f"raw{u}_{i}", align_bytes=64) for i, (tokens, helper) in enumerate(PIECES[u])]
-            for u in range(4)
+            for u in range(1, 4)
         ]
+        raw0 = keep.tile([P, 2, T], F32, name="raw0", align_bytes=64)
+        raws = [[raw0[:, :, : T // 2], raw0[:, :, T // 2 :]]] + raws
         pairs = [keep.tile([P, T, 2], BF16, name=f"pairs{u}", align_bytes=64) for u in range(4)]
         picked1 = keep.tile([P, 2, S], U32, name="picked1", align_bytes=64)
         picked0 = keep.tile([P, 2, S], U32, name="picked0", align_bytes=64)
@@ -79,7 +81,8 @@ def tile_moe_res_lin_relu_kernel(
         banks = [psum.tile([P, GROUP], F32, name=f"bank{n}") for n in range(S // GROUP)]
 
         nc.gpsimd.memset(w_scales[:].rearrange("p e n -> p (e n)").bitcast(I32), 0)
-        nc.vector.memset(routed[:], 0.0)
+        nc.vector.memset(routed[:, : T // 2], 0.0)
+        nc.scalar.activation(routed[:, T // 2 :], routed[:, : T // 2], COPY)
 
         def first_token(u, i):
             return sum(tokens for tokens, helper in PIECES[u][:i])
@@ -97,7 +100,10 @@ def tile_moe_res_lin_relu_kernel(
                     scales[:, 0, 4 * quadrant : 4 * quadrant + 4, :].rearrange("e q n -> q e n").bitcast(I32),
                 )
 
-        load_x(0, 0)
+        first_rows = xT[:PASS, :].rearrange("(p t) w -> p t w", t=4)
+        nc.sync.dma_start(raw0[:, 0, :], first_rows[:, 0, :])
+        nc.sync.dma_start(raw0[:, 1, : T // 2], first_rows[:, 1, : T // 2])
+        nc.sync.dma_start(raw0[:, 1, T // 2 :], first_rows[:, 1, T // 2 :])
         nc.sync.dma_start(offsets[:], offs)
         for u in range(1, 4):
             for i in range(len(PIECES[u])):

@@ -37,10 +37,8 @@ GPSIMD_WEAVES = ((0, 192), (192, HALF))
 VECTOR_WEAVE = (HALF, S)
 
 SCATTERS = ((0, 1), (1, E))
-FIRST_CUT, LATER_CUTS = 256, 4
-CUTS = ((0, FIRST_CUT),) + tuple(
-    (FIRST_CUT + i * (T - FIRST_CUT) // LATER_CUTS, FIRST_CUT + (i + 1) * (T - FIRST_CUT) // LATER_CUTS) for i in range(LATER_CUTS)
-)
+CUT = 256
+CUTS = tuple((lo, lo + CUT) for lo in range(0, T, CUT))
 
 FIRST8, FIRST4 = 4, 0
 
@@ -100,10 +98,11 @@ def tile_moe_res_lin_relu_kernel(
                     scales[:, 0, 4 * quadrant : 4 * quadrant + 4, :].rearrange("e q n -> q e n").bitcast(I32),
                 )
 
-        first_rows = xT[:PASS, :].rearrange("(p t) w -> p t w", t=4)
-        nc.sync.dma_start(raw0[:, 0, :], first_rows[:, 0, :])
-        nc.sync.dma_start(raw0[:, 1, : T // 2], first_rows[:, 1, : T // 2])
-        nc.sync.dma_start(raw0[:, 1, T // 2 :], first_rows[:, 1, T // 2 :])
+        first_rows = xT[:PASS, :].rearrange("(p t) w -> p (t w)", t=4)
+        raw0_rows = raw0[:].rearrange("p j c -> p (j c)")
+        joint = T + PIECES[0][0][0]
+        nc.sync.dma_start(raw0_rows[:, :joint], first_rows[:, :joint])
+        nc.sync.dma_start(raw0_rows[:, joint:], first_rows[:, joint : 2 * T])
         nc.sync.dma_start(offsets[:], offs)
         for u in range(1, 4):
             for i in range(len(PIECES[u])):

@@ -112,7 +112,8 @@ def tile_moe_res_lin_relu_kernel(
         nc.sync.dma_start(w4[:].bitcast(I32), w4_words.rearrange("e a p m -> p (e a) m").bitcast(I32))
         load_scale_rows(w4_scales, FIRST4)
         nc.sync.dma_start(bias[:], b)
-        nc.sync.dma_start(gates[:], gate)
+        nc.sync.dma_start(gates[:, :C], gate[:, :C])
+        nc.sync.dma_start(gates[:, C:], gate[:, C:])
         nc.sync.dma_start(resid[:], xr)
 
         def side_by_side(two_rows):
@@ -188,7 +189,9 @@ def tile_moe_res_lin_relu_kernel(
             gather(picked1, 3, e * C, (e + 1) * C)
             nc.scalar.copy(woven1[e][:], side_by_side(picked1[:, :, e * C : (e + 1) * C]))
         for e in range(E):
-            quantise(codes1[e][:], scales1[e][:], woven1[e][:])
+            step = GROUP if e == 0 else C
+            for lo in range(0, C, step):
+                quantise(codes1[e][:, lo : lo + step], scales1[e][:, lo : lo + step], woven1[e][:, lo : lo + step, :])
             open_sums(e)
             close_sums(e)
 

@@ -36,11 +36,11 @@ HALF = S // 2
 GPSIMD_WEAVES = ((0, 192), (192, HALF))
 VECTOR_WEAVE = (HALF, S)
 
+LAST_STEPS = ((0, 256), (256, 544), (544, 832), (832, S))
+
 SCATTERS = ((0, 1), (1, E))
 CUT = 256
 CUTS = tuple((lo, lo + CUT) for lo in range(0, T, CUT))
-
-FIRST8, FIRST4 = 4, 0
 
 
 def tile_moe_res_lin_relu_kernel(
@@ -62,14 +62,15 @@ def tile_moe_res_lin_relu_kernel(
         picked1 = keep.tile([P, 2, S], U32, name="picked1", align_bytes=64)
         picked0 = keep.tile([P, 2, S], U32, name="picked0", align_bytes=64)
         woven0 = keep.tile([P, S, 2], U32, name="woven0", align_bytes=64)
-        woven1 = [keep.tile([P, C, 2], U32, name=f"woven1_{e}", align_bytes=64) for e in range(E)]
+        woven1 = keep.tile([P, S, 2], U32, name="woven1", align_bytes=64)
         codes0 = keep.tile([P, S], U32, name="codes0", align_bytes=64)
         scales0 = keep.tile([P, S], U8, name="scales0", align_bytes=64)
         codes1 = [keep.tile([P, C], U32, name=f"codes1_{e}", align_bytes=64) for e in range(E)]
         scales1 = [keep.tile([P, C], U8, name=f"scales1_{e}", align_bytes=64) for e in range(E)]
         w8 = keep.tile([P, E, 4 * N], U8, name="w8", align_bytes=64)
         w4 = keep.tile([P, E, 2 * N], U8, name="w4", align_bytes=64)
-        w_scales = keep.tile([P, E, N], U8, name="w_scales", align_bytes=64)
+        w8_rows = keep.tile([P, E, N], U8, name="w8_rows", align_bytes=64)
+        w4_rows = keep.tile([P, E, N], U8, name="w4_rows", align_bytes=64)
         bias = keep.tile([P, E], F32, name="bias")
         gates = keep.tile([P, S], F32, name="gates")
         resid = keep.tile([P, T], F32, name="resid")
@@ -78,7 +79,8 @@ def tile_moe_res_lin_relu_kernel(
         sums = [keep.tile([P, hi - lo], F32, name=f"sum{i}") for i, (lo, hi) in enumerate(CUTS)]
         banks = [psum.tile([P, GROUP], F32, name=f"bank{n}") for n in range(S // GROUP)]
 
-        nc.gpsimd.memset(w_scales[:].rearrange("p e n -> p (e n)").bitcast(I32), 0)
+        for rows in (w8_rows, w4_rows):
+            nc.gpsimd.memset(rows[:].rearrange("p e n -> p (e n)").bitcast(I32), 0)
         nc.vector.memset(routed[:, : T // 2], 0.0)
         nc.scalar.activation(routed[:, T // 2 :], routed[:, : T // 2], COPY)
 
@@ -91,10 +93,10 @@ def tile_moe_res_lin_relu_kernel(
             rows = xT[PASS * a : PASS * (a + 1), start : start + PIECES[u][i][0]].rearrange("(p t) w -> p t w", t=4)
             nc.sync.dma_start(raws[u][i][:], rows[:, 2 * h : 2 * h + 2, :])
 
-        def load_scale_rows(scales, first):
+        def load_scale_rows(rows, scales):
             for quadrant in range(4):
                 nc.sync.dma_start(
-                    w_scales[32 * quadrant + first : 32 * quadrant + first + 4, :, :].bitcast(I32),
+                    rows[32 * quadrant : 32 * quadrant + 4, :, :].bitcast(I32),
                     scales[:, 0, 4 * quadrant : 4 * quadrant + 4, :].rearrange("e q n -> q e n").bitcast(I32),
                 )
 
@@ -108,9 +110,9 @@ def tile_moe_res_lin_relu_kernel(
             for i in range(len(PIECES[u])):
                 load_x(u, i)
         nc.sync.dma_start(w8[:].bitcast(I32), w8_words.rearrange("e a p n t -> p (e a) (n t)").bitcast(I32))
-        load_scale_rows(w8_scales, FIRST8)
+        load_scale_rows(w8_rows, w8_scales)
         nc.sync.dma_start(w4[:].bitcast(I32), w4_words.rearrange("e a p m -> p (e a) m").bitcast(I32))
-        load_scale_rows(w4_scales, FIRST4)
+        load_scale_rows(w4_rows, w4_scales)
         nc.sync.dma_start(bias[:], b)
         nc.sync.dma_start(gates[:, :C], gate[:, :C])
         nc.sync.dma_start(gates[:, C:], gate[:, C:])
@@ -148,7 +150,7 @@ def tile_moe_res_lin_relu_kernel(
                 nc.tensor.matmul_mx(
                     out=banks[n][:],
                     lhsT=w8[:, e, :].bitcast(FP8X4),
-                    lhsT_scale=w_scales[FIRST8:P, e, :],
+                    lhsT_scale=w8_rows[:, e, :],
                     rhs=codes0[:, slots].bitcast(FP8X4),
                     rhs_scale=scales0[:, slots],
                     start=True,
@@ -162,7 +164,7 @@ def tile_moe_res_lin_relu_kernel(
                 nc.tensor.matmul_mx(
                     out=banks[2 * e + half][:],
                     lhsT=w4[:, e, :].bitcast(FP4X4),
-                    lhsT_scale=w_scales[FIRST4:P, e, :],
+                    lhsT_scale=w4_rows[:, e, :],
                     rhs=codes1[e][:, places].bitcast(FP8X4),
                     rhs_scale=scales1[e][:, places],
                     start=False,
@@ -182,17 +184,19 @@ def tile_moe_res_lin_relu_kernel(
         for lo in (0, HALF):
             quantise(codes0[:, lo : lo + HALF], scales0[:, lo : lo + HALF], woven0[:, lo : lo + HALF, :])
 
+        for e in range(E):
+            open_sums(e)
+
         round_pair(2)
         gather(picked1, 2, 0, S)
         round_pair(3)
-        for e in range(E):
-            gather(picked1, 3, e * C, (e + 1) * C)
-            nc.scalar.copy(woven1[e][:], side_by_side(picked1[:, :, e * C : (e + 1) * C]))
+        for lo, hi in LAST_STEPS:
+            gather(picked1, 3, lo, hi)
+            nc.scalar.copy(woven1[:, lo:hi, :], side_by_side(picked1[:, :, lo:hi]))
         for e in range(E):
             step = GROUP if e == 0 else C
             for lo in range(0, C, step):
-                quantise(codes1[e][:, lo : lo + step], scales1[e][:, lo : lo + step], woven1[e][:, lo : lo + step, :])
-            open_sums(e)
+                quantise(codes1[e][:, lo : lo + step], scales1[e][:, lo : lo + step], woven1[:, e * C + lo : e * C + lo + step, :])
             close_sums(e)
 
         for g, (lo, hi) in enumerate(SCATTERS):

@@ -27,9 +27,9 @@ PIECES = (
     ((768, "vector"), (768, "vector")),
     ((896, "gpsimd"), (640, "vector")),
     ((768, "none"), (768, "none")),
-    ((768, "gpsimd"), (512, "gpsimd"), (256, "gpsimd")),
+    ((768, "idle gpsimd"), (512, "gpsimd"), (256, "gpsimd")),
 )
-SCALAR_SHARE = {"vector": 9, "gpsimd": 16, "none": 24}
+SCALAR_SHARE = {"vector": 9, "gpsimd": 16, "idle gpsimd": 13, "none": 24}
 SHARE_STEP = 16
 
 HALF = S // 2

@@ -14,12 +14,12 @@ MULT = mybir.AluOpType.mult
 ADD = mybir.AluOpType.add
 COPY = mybir.ActivationFunctionType.Copy
 RELU = mybir.ActivationFunctionType.Relu
+MAX = mybir.AluOpType.max
 
 P = 128
 K, T, E, C, N = 1024, 1536, 4, 256, 128
 S = E * C
 PASS = 512
-GROUP = 128
 LIST = 16
 FLOPS = 2 * E * C * K * N
 
@@ -36,9 +36,8 @@ HALF = S // 2
 GPSIMD_WEAVES = ((0, 192), (192, HALF))
 VECTOR_WEAVE = (HALF, S)
 
-LAST_STEPS = ((0, 256), (256, 544), (544, 832), (832, S))
-
-SCATTERS = ((0, 1), (1, E))
+SCALAR_SCATTERS = ((0, C), (C, 2 * C), (2 * C, 832))
+VECTOR_SCATTER = (832, S)
 CUT = 256
 CUTS = tuple((lo, lo + CUT) for lo in range(0, T, CUT))
 
@@ -59,30 +58,39 @@ def tile_moe_res_lin_relu_kernel(
         raw0 = keep.tile([P, 2, T], F32, name="raw0", align_bytes=64)
         raws = [[raw0[:, :, : T // 2], raw0[:, :, T // 2 :]]] + raws
         pairs = [keep.tile([P, T, 2], BF16, name=f"pairs{u}", align_bytes=64) for u in range(4)]
-        picked1 = keep.tile([P, 2, S], U32, name="picked1", align_bytes=64)
+        picked1 = keep.tile([P, 7, C], U32, name="picked1", align_bytes=64)
         picked0 = keep.tile([P, 2, S], U32, name="picked0", align_bytes=64)
         woven0 = keep.tile([P, S, 2], U32, name="woven0", align_bytes=64)
-        woven1 = keep.tile([P, S, 2], U32, name="woven1", align_bytes=64)
+        woven1 = [keep.tile([P, C, 2], U32, name=f"woven1_{e}", align_bytes=64)[:] for e in range(E - 1)]
+        woven_last = keep.tile([P, 2 * C + E - 1], U32, name="woven_last", align_bytes=64)
+        woven1.append(woven_last[:, : 2 * C].rearrange("p (s h) -> p s h", h=2))
         codes0 = keep.tile([P, S], U32, name="codes0", align_bytes=64)
         scales0 = keep.tile([P, S], U8, name="scales0", align_bytes=64)
-        codes1 = [keep.tile([P, C], U32, name=f"codes1_{e}", align_bytes=64) for e in range(E)]
+        codes1 = {e: keep.tile([P, C], U32, name=f"codes1_{e}", align_bytes=64) for e in (0, 1, 3)}
+        y0 = keep.tile([P, C], F32, name="y0", tag="y0_then_codes", align_bytes=64)
         scales1 = [keep.tile([P, C], U8, name=f"scales1_{e}", align_bytes=64) for e in range(E)]
         w8 = keep.tile([P, E, 4 * N], U8, name="w8", align_bytes=64)
         w4 = keep.tile([P, E, 2 * N], U8, name="w4", align_bytes=64)
         w8_rows = keep.tile([P, E, N], U8, name="w8_rows", align_bytes=64)
         w4_rows = keep.tile([P, E, N], U8, name="w4_rows", align_bytes=64)
-        bias = keep.tile([P, E], F32, name="bias")
+        bias = woven_last[:, 2 * C - 1 :].bitcast(F32)
         gates = keep.tile([P, S], F32, name="gates")
         resid = keep.tile([P, T], F32, name="resid")
-        ys = [keep.tile([P, (hi - lo) * C], F32, name=f"y{g}") for g, (lo, hi) in enumerate(SCATTERS)]
-        routed = keep.tile([P, T], F32, name="routed")
+        y1 = keep.tile([P, C], F32, name="y1")
+        y23 = keep.tile([P, HALF], F32, name="y23")
+        ys = [y0[:], y1[:], y23[:, :C], y23[:, C:]]
+        gated = [keep.tile([P, hi - lo], F32, name=f"gated{i}") for i, (lo, hi) in enumerate(SCALAR_SCATTERS)]
+        routed_s = keep.tile([P, T], F32, name="routed_s")
+        routed_v = keep.tile([P, T], F32, name="routed_v")
+        partial = keep.tile([P, T], F32, name="partial")
         sums = [keep.tile([P, hi - lo], F32, name=f"sum{i}") for i, (lo, hi) in enumerate(CUTS)]
-        banks = [psum.tile([P, GROUP], F32, name=f"bank{n}") for n in range(S // GROUP)]
+        banks = [psum.tile([P, C], F32, name=f"bank{e}") for e in range(E)]
 
         for rows in (w8_rows, w4_rows):
             nc.gpsimd.memset(rows[:].rearrange("p e n -> p (e n)").bitcast(I32), 0)
-        nc.vector.memset(routed[:, : T // 2], 0.0)
-        nc.scalar.activation(routed[:, T // 2 :], routed[:, : T // 2], COPY)
+        nc.vector.memset(routed_s[:, : T // 2], 0.0)
+        nc.scalar.activation(routed_s[:, T // 2 :], routed_s[:, : T // 2], COPY)
+        nc.vector.memset(routed_v[:], 0.0)
 
         def first_token(u, i):
             return sum(tokens for tokens, helper in PIECES[u][:i])
@@ -109,12 +117,12 @@ def tile_moe_res_lin_relu_kernel(
         for u in range(1, 4):
             for i in range(len(PIECES[u])):
                 load_x(u, i)
-        nc.sync.dma_start(w8[:].bitcast(I32), w8_words.rearrange("e a p n t -> p (e a) (n t)").bitcast(I32))
-        load_scale_rows(w8_rows, w8_scales)
-        nc.sync.dma_start(w4[:].bitcast(I32), w4_words.rearrange("e a p m -> p (e a) m").bitcast(I32))
         load_scale_rows(w4_rows, w4_scales)
-        nc.sync.dma_start(bias[:], b)
+        nc.sync.dma_start(w4[:].bitcast(I32), w4_words.rearrange("e a p m -> p (e a) m").bitcast(I32))
+        nc.sync.dma_start(w8[:].bitcast(I32), w8_words.rearrange("e a p n t -> p (e a) (n t)").bitcast(I32))
         nc.sync.dma_start(gates[:, :C], gate[:, :C])
+        load_scale_rows(w8_rows, w8_scales)
+        nc.sync.dma_start(bias, b)
         nc.sync.dma_start(gates[:, C:], gate[:, C:])
         nc.sync.dma_start(resid[:], xr)
 
@@ -132,7 +140,7 @@ def tile_moe_res_lin_relu_kernel(
 
         def gather(picked, u, lo, hi):
             window = pairs[u][:].rearrange("p t j -> p (t j)").bitcast(U32)
-            nc.vector.tensor_copy(picked[:, u % 2, lo:hi], window.indirect(offsets[:, lo // LIST : hi // LIST]))
+            nc.vector.tensor_copy(picked, window.indirect(offsets[:, lo // LIST : hi // LIST]))
 
         def weave0(engine, lo, hi):
             engine.tensor_copy(woven0[:, lo:hi, :].bitcast(I32), side_by_side(picked0[:, :, lo:hi].bitcast(I32)))
@@ -144,64 +152,84 @@ def tile_moe_res_lin_relu_kernel(
                 in_=woven.rearrange("p s h -> p (s h)").bitcast(BF16),
             )
 
-        def open_sums(e):
-            for n in (2 * e, 2 * e + 1):
-                slots = slice(n * GROUP, (n + 1) * GROUP)
-                nc.tensor.matmul_mx(
-                    out=banks[n][:],
-                    lhsT=w8[:, e, :].bitcast(FP8X4),
-                    lhsT_scale=w8_rows[:, e, :],
-                    rhs=codes0[:, slots].bitcast(FP8X4),
-                    rhs_scale=scales0[:, slots],
-                    start=True,
-                    stop=False,
-                )
-
-        def close_sums(e):
-            g = 0 if e < SCATTERS[0][1] else 1
-            for half in range(2):
-                places = slice(half * GROUP, (half + 1) * GROUP)
-                nc.tensor.matmul_mx(
-                    out=banks[2 * e + half][:],
-                    lhsT=w4[:, e, :].bitcast(FP4X4),
-                    lhsT_scale=w4_rows[:, e, :],
-                    rhs=codes1[e][:, places].bitcast(FP8X4),
-                    rhs_scale=scales1[e][:, places],
-                    start=False,
-                    stop=True,
-                )
-                at = (e - SCATTERS[g][0]) * C + half * GROUP
-                nc.scalar.activation(ys[g][:, at : at + GROUP], banks[2 * e + half][:], RELU, bias=bias[:, e : e + 1])
+        def product(e, a):
+            slots = slice(e * C, (e + 1) * C)
+            nc.tensor.matmul_mx(
+                out=banks[e][:],
+                lhsT=w8[:, e, :].bitcast(FP8X4) if a == 0 else w4[:, e, :].bitcast(FP4X4),
+                lhsT_scale=(w8_rows, w4_rows)[a][:, e, :],
+                rhs=(codes0[:, slots] if a == 0 else codes1[e][:]).bitcast(FP8X4),
+                rhs_scale=scales0[:, slots] if a == 0 else scales1[e][:],
+                start=a == 0,
+                stop=a == 1,
+            )
 
         round_pair(0)
-        gather(picked0, 0, 0, S)
+        gather(picked0[:, 0, :], 0, 0, S)
         round_pair(1)
         for lo, hi in GPSIMD_WEAVES + (VECTOR_WEAVE,):
-            gather(picked0, 1, lo, hi)
+            gather(picked0[:, 1, lo:hi], 1, lo, hi)
         for lo, hi in GPSIMD_WEAVES:
             weave0(nc.gpsimd, lo, hi)
         weave0(nc.vector, *VECTOR_WEAVE)
         for lo in (0, HALF):
             quantise(codes0[:, lo : lo + HALF], scales0[:, lo : lo + HALF], woven0[:, lo : lo + HALF, :])
 
-        for e in range(E):
-            open_sums(e)
-
+        blocks = (picked1[:, 0:3:2, :], picked1[:, 3:6:2, :], picked1[:, 1:3, :], picked1[:, 4:7:2, :])
         round_pair(2)
-        gather(picked1, 2, 0, S)
+        early = picked1[:, :6, :].rearrange("p (b a) c -> p a b c", a=3)
+        gather(early[:, :2, :, :], 2, 0, S)
         round_pair(3)
-        for lo, hi in LAST_STEPS:
-            gather(picked1, 3, lo, hi)
-            nc.scalar.copy(woven1[:, lo:hi, :], side_by_side(picked1[:, :, lo:hi]))
-        for e in range(E):
-            step = GROUP if e == 0 else C
-            for lo in range(0, C, step):
-                quantise(codes1[e][:, lo : lo + step], scales1[e][:, lo : lo + step], woven1[:, e * C + lo : e * C + lo + step, :])
-            close_sums(e)
 
-        for g, (lo, hi) in enumerate(SCATTERS):
-            window = routed[:].indirect(offsets[:, lo * C // LIST : hi * C // LIST])
-            nc.vector.tensor_tensor(window, ys[g][:], gates[:, lo * C : hi * C], MULT)
+        def offsets_of(lo, hi):
+            return offsets[:, lo // LIST : hi // LIST]
+
+        def late(e, lo, hi):
+            gather(blocks[e][:, 1, lo:hi], 3, e * C + lo, e * C + hi)
+            if e < 2:
+                nc.scalar.copy(woven1[e][:, lo:hi, :], side_by_side(blocks[e][:, :, lo:hi]))
+            elif e == 2:
+                nc.gpsimd.tensor_copy(woven1[e][:, lo:hi, :], side_by_side(blocks[e][:, :, lo:hi]))
+
+
+        def close(e):
+            quantise(codes1[e][:], scales1[e][:], woven1[e])
+            product(e, 0)
+            product(e, 1)
+
+        def relu(e):
+            if e < 2:
+                nc.scalar.activation(ys[e], banks[e][:], RELU, bias=bias[:, e : e + 1])
+            else:
+                nc.vector.tensor_scalar(ys[e], banks[e][:], bias[:, e : e + 1], 0.0, ADD, MAX)
+
+        def send_back(i):
+            lo, hi = SCALAR_SCATTERS[i]
+            results = ys[i] if i < 2 else y23[:, : hi - lo]
+            nc.vector.tensor_tensor(gated[i][:], results, gates[:, lo:hi], MULT)
+            nc.scalar.activation(routed_s[:].indirect(offsets_of(lo, hi)), gated[i][:], COPY)
+
+        late(0, 0, C // 2)
+        late(0, C // 2, C)
+        late(1, 0, C)
+        close(0)
+        relu(0)
+        late(2, 0, C)
+        close(1)
+        relu(1)
+        late(3, 0, C)
+        send_back(0)
+        nc.vector.tensor_copy(woven1[3].bitcast(I32), side_by_side(blocks[3].bitcast(I32)))
+        codes1[2] = keep.tile([P, C], U32, name="codes1_2", tag="y0_then_codes", align_bytes=64)
+        close(2)
+        close(3)
+        send_back(1)
+        relu(2)
+        relu(3)
+        send_back(2)
+        lo, hi = VECTOR_SCATTER
+        nc.vector.tensor_tensor(routed_v[:].indirect(offsets_of(lo, hi)), y23[:, lo - HALF :], gates[:, lo:hi], MULT)
+        nc.vector.tensor_tensor(partial[:], routed_v[:], resid[:], ADD)
         for i, (lo, hi) in enumerate(CUTS):
-            nc.vector.tensor_tensor(sums[i][:], routed[:, lo:hi], resid[:, lo:hi], ADD)
+            nc.vector.tensor_tensor(sums[i][:], routed_s[:, lo:hi], partial[:, lo:hi], ADD)
             nc.sync.dma_start(out[:, lo:hi], sums[i][:])

@@ -36,8 +36,8 @@ HALF = S // 2
 GPSIMD_WEAVES = ((0, 192), (192, HALF))
 VECTOR_WEAVE = (HALF, S)
 
-SCALAR_SCATTERS = ((0, C), (C, 2 * C), (2 * C, 832))
-VECTOR_SCATTER = (832, S)
+SCALAR_SCATTERS = ((0, C), (C, 2 * C), (736, S))
+VECTOR_SCATTER = (2 * C, 736)
 CUT = 256
 CUTS = tuple((lo, lo + CUT) for lo in range(0, T, CUT))
 
@@ -61,13 +61,12 @@ def tile_moe_res_lin_relu_kernel(
         picked1 = keep.tile([P, 7, C], U32, name="picked1", align_bytes=64)
         picked0 = keep.tile([P, 2, S], U32, name="picked0", align_bytes=64)
         woven0 = keep.tile([P, S, 2], U32, name="woven0", align_bytes=64)
-        woven1 = [keep.tile([P, C, 2], U32, name=f"woven1_{e}", align_bytes=64)[:] for e in range(E - 1)]
+        woven1 = {e: keep.tile([P, C, 2], U32, name=f"woven1_{e}", align_bytes=64)[:] for e in (0, 1, 3)}
         woven_last = keep.tile([P, 2 * C + E - 1], U32, name="woven_last", align_bytes=64)
-        woven1.append(woven_last[:, : 2 * C].rearrange("p (s h) -> p s h", h=2))
+        woven1[2] = woven_last[:, : 2 * C].rearrange("p (s h) -> p s h", h=2)
         codes0 = keep.tile([P, S], U32, name="codes0", align_bytes=64)
         scales0 = keep.tile([P, S], U8, name="scales0", align_bytes=64)
-        codes1 = {e: keep.tile([P, C], U32, name=f"codes1_{e}", align_bytes=64) for e in (0, 1, 3)}
-        y0 = keep.tile([P, C], F32, name="y0", tag="y0_then_codes", align_bytes=64)
+        codes1 = [keep.tile([P, C], U32, name=f"codes1_{e}", align_bytes=64) for e in range(E)]
         scales1 = [keep.tile([P, C], U8, name=f"scales1_{e}", align_bytes=64) for e in range(E)]
         w8 = keep.tile([P, E, 4 * N], U8, name="w8", align_bytes=64)
         w4 = keep.tile([P, E, 2 * N], U8, name="w4", align_bytes=64)
@@ -76,9 +75,6 @@ def tile_moe_res_lin_relu_kernel(
         bias = woven_last[:, 2 * C - 1 :].bitcast(F32)
         gates = keep.tile([P, S], F32, name="gates")
         resid = keep.tile([P, T], F32, name="resid")
-        y1 = keep.tile([P, C], F32, name="y1")
-        y23 = keep.tile([P, HALF], F32, name="y23")
-        ys = [y0[:], y1[:], y23[:, :C], y23[:, C:]]
         gated = [keep.tile([P, hi - lo], F32, name=f"gated{i}") for i, (lo, hi) in enumerate(SCALAR_SCATTERS)]
         routed_s = keep.tile([P, T], F32, name="routed_s")
         routed_v = keep.tile([P, T], F32, name="routed_v")
@@ -186,49 +182,43 @@ def tile_moe_res_lin_relu_kernel(
 
         def late(e, lo, hi):
             gather(blocks[e][:, 1, lo:hi], 3, e * C + lo, e * C + hi)
-            if e < 2:
-                nc.scalar.copy(woven1[e][:, lo:hi, :], side_by_side(blocks[e][:, :, lo:hi]))
-            elif e == 2:
-                nc.gpsimd.tensor_copy(woven1[e][:, lo:hi, :], side_by_side(blocks[e][:, :, lo:hi]))
-
+            nc.scalar.copy(woven1[e][:, lo:hi, :], side_by_side(blocks[e][:, :, lo:hi]))
 
         def close(e):
             quantise(codes1[e][:], scales1[e][:], woven1[e])
             product(e, 0)
             product(e, 1)
 
-        def relu(e):
-            if e < 2:
-                nc.scalar.activation(ys[e], banks[e][:], RELU, bias=bias[:, e : e + 1])
-            else:
-                nc.vector.tensor_scalar(ys[e], banks[e][:], bias[:, e : e + 1], 0.0, ADD, MAX)
-
-        def send_back(i):
+        def send_back(i, results):
             lo, hi = SCALAR_SCATTERS[i]
-            results = ys[i] if i < 2 else y23[:, : hi - lo]
             nc.vector.tensor_tensor(gated[i][:], results, gates[:, lo:hi], MULT)
             nc.scalar.activation(routed_s[:].indirect(offsets_of(lo, hi)), gated[i][:], COPY)
 
         late(0, 0, C // 2)
         late(0, C // 2, C)
         late(1, 0, C)
+        late(3, 0, C)
         close(0)
-        relu(0)
+        y0 = keep.tile([P, C], F32, name="y0", tag="results")
+        nc.scalar.activation(y0[:], banks[0][:], RELU, bias=bias[:, 0:1])
         late(2, 0, C)
         close(1)
-        relu(1)
-        late(3, 0, C)
-        send_back(0)
-        nc.vector.tensor_copy(woven1[3].bitcast(I32), side_by_side(blocks[3].bitcast(I32)))
-        codes1[2] = keep.tile([P, C], U32, name="codes1_2", tag="y0_then_codes", align_bytes=64)
-        close(2)
         close(3)
-        send_back(1)
-        relu(2)
+        send_back(0, y0[:])
+        rest = keep.tile([P, S - C], F32, name="rest", tag="results")
+
+        def relu(e):
+            nc.vector.tensor_scalar(rest[:, (e - 1) * C : e * C], banks[e][:], bias[:, e : e + 1], 0.0, ADD, MAX)
+
+        relu(1)
+        close(2)
         relu(3)
-        send_back(2)
+        send_back(1, rest[:, :C])
+        relu(2)
+        send_back(2, rest[:, SCALAR_SCATTERS[2][0] - C :])
         lo, hi = VECTOR_SCATTER
-        nc.vector.tensor_tensor(routed_v[:].indirect(offsets_of(lo, hi)), y23[:, lo - HALF :], gates[:, lo:hi], MULT)
+        window = routed_v[:].indirect(offsets_of(lo, hi))
+        nc.vector.tensor_tensor(window, rest[:, lo - C : hi - C], gates[:, lo:hi], MULT)
         nc.vector.tensor_tensor(partial[:], routed_v[:], resid[:], ADD)
         for i, (lo, hi) in enumerate(CUTS):
             nc.vector.tensor_tensor(sums[i][:], routed_s[:, lo:hi], partial[:, lo:hi], ADD)

@@ -36,8 +36,8 @@ HALF = S // 2
 GPSIMD_WEAVES = ((0, 192), (192, HALF))
 VECTOR_WEAVE = (HALF, S)
 
-SCALAR_SCATTERS = ((0, C), (C, 2 * C), (736, S))
-VECTOR_SCATTER = (2 * C, 736)
+SCALAR_SCATTERS = ((0, C), (C, 2 * C), (800, S))
+VECTOR_SCATTER = (2 * C, 800)
 CUT = 256
 CUTS = tuple((lo, lo + CUT) for lo in range(0, T, CUT))
 
@@ -214,8 +214,8 @@ def tile_moe_res_lin_relu_kernel(
         close(2)
         relu(3)
         send_back(1, rest[:, :C])
-        relu(2)
         send_back(2, rest[:, SCALAR_SCATTERS[2][0] - C :])
+        relu(2)
         lo, hi = VECTOR_SCATTER
         window = routed_v[:].indirect(offsets_of(lo, hi))
         nc.vector.tensor_tensor(window, rest[:, lo - C : hi - C], gates[:, lo:hi], MULT)

@@ -36,8 +36,7 @@ HALF = S // 2
 GPSIMD_WEAVES = ((0, 192), (192, HALF))
 VECTOR_WEAVE = (HALF, S)
 
-SCALAR_SCATTERS = ((0, C), (C, 2 * C), (800, S))
-VECTOR_SCATTER = (2 * C, 800)
+ORDER = (0, 2, 3, 1)
 CUT = 256
 CUTS = tuple((lo, lo + CUT) for lo in range(0, T, CUT))
 
@@ -61,9 +60,9 @@ def tile_moe_res_lin_relu_kernel(
         picked1 = keep.tile([P, 7, C], U32, name="picked1", align_bytes=64)
         picked0 = keep.tile([P, 2, S], U32, name="picked0", align_bytes=64)
         woven0 = keep.tile([P, S, 2], U32, name="woven0", align_bytes=64)
-        woven1 = {e: keep.tile([P, C, 2], U32, name=f"woven1_{e}", align_bytes=64)[:] for e in (0, 1, 3)}
+        woven1 = {e: keep.tile([P, C, 2], U32, name=f"woven1_{e}", align_bytes=64)[:] for e in ORDER[:3]}
         woven_last = keep.tile([P, 2 * C + E - 1], U32, name="woven_last", align_bytes=64)
-        woven1[2] = woven_last[:, : 2 * C].rearrange("p (s h) -> p s h", h=2)
+        woven1[1] = woven_last[:, : 2 * C].rearrange("p (s h) -> p s h", h=2)
         codes0 = keep.tile([P, S], U32, name="codes0", align_bytes=64)
         scales0 = keep.tile([P, S], U8, name="scales0", align_bytes=64)
         codes1 = [keep.tile([P, C], U32, name=f"codes1_{e}", align_bytes=64) for e in range(E)]
@@ -75,7 +74,7 @@ def tile_moe_res_lin_relu_kernel(
         bias = woven_last[:, 2 * C - 1 :].bitcast(F32)
         gates = keep.tile([P, S], F32, name="gates")
         resid = keep.tile([P, T], F32, name="resid")
-        gated = [keep.tile([P, hi - lo], F32, name=f"gated{i}") for i, (lo, hi) in enumerate(SCALAR_SCATTERS)]
+        gated = {e: keep.tile([P, C], F32, name=f"gated{e}") for e in ORDER[:3]}
         routed_s = keep.tile([P, T], F32, name="routed_s")
         routed_v = keep.tile([P, T], F32, name="routed_v")
         partial = keep.tile([P, T], F32, name="partial")
@@ -171,14 +170,15 @@ def tile_moe_res_lin_relu_kernel(
         for lo in (0, HALF):
             quantise(codes0[:, lo : lo + HALF], scales0[:, lo : lo + HALF], woven0[:, lo : lo + HALF, :])
 
-        blocks = (picked1[:, 0:3:2, :], picked1[:, 3:6:2, :], picked1[:, 1:3, :], picked1[:, 4:7:2, :])
+        blocks = (picked1[:, 0:3:2, :], picked1[:, 1:3, :], picked1[:, 3:6:2, :], picked1[:, 4:7:2, :])
         round_pair(2)
-        early = picked1[:, :6, :].rearrange("p (b a) c -> p a b c", a=3)
-        gather(early[:, :2, :, :], 2, 0, S)
+        for half in range(2):
+            early = picked1[:, 3 * half : 3 * half + 2, :].rearrange("p e c -> p (e c)")
+            gather(early, 2, half * HALF, (half + 1) * HALF)
         round_pair(3)
 
-        def offsets_of(lo, hi):
-            return offsets[:, lo // LIST : hi // LIST]
+        def offsets_of(e):
+            return offsets[:, e * C // LIST : (e + 1) * C // LIST]
 
         def late(e, lo, hi):
             gather(blocks[e][:, 1, lo:hi], 3, e * C + lo, e * C + hi)
@@ -189,36 +189,35 @@ def tile_moe_res_lin_relu_kernel(
             product(e, 0)
             product(e, 1)
 
-        def send_back(i, results):
-            lo, hi = SCALAR_SCATTERS[i]
-            nc.vector.tensor_tensor(gated[i][:], results, gates[:, lo:hi], MULT)
-            nc.scalar.activation(routed_s[:].indirect(offsets_of(lo, hi)), gated[i][:], COPY)
+        def send_back(e, results):
+            nc.vector.tensor_tensor(gated[e][:], results, gates[:, e * C : (e + 1) * C], MULT)
+            nc.scalar.activation(routed_s[:].indirect(offsets_of(e)), gated[e][:], COPY)
 
-        late(0, 0, C // 2)
-        late(0, C // 2, C)
-        late(1, 0, C)
-        late(3, 0, C)
-        close(0)
-        y0 = keep.tile([P, C], F32, name="y0", tag="results")
-        nc.scalar.activation(y0[:], banks[0][:], RELU, bias=bias[:, 0:1])
-        late(2, 0, C)
-        close(1)
-        close(3)
-        send_back(0, y0[:])
-        rest = keep.tile([P, S - C], F32, name="rest", tag="results")
+        first, second, third, last = ORDER
+        late(first, 0, C // 2)
+        late(first, C // 2, C)
+        late(second, 0, C)
+        late(third, 0, C)
+        close(first)
+        y_first = keep.tile([P, C], F32, name="y_first", tag="results")
+        nc.scalar.activation(y_first[:], banks[first][:], RELU, bias=bias[:, first : first + 1])
+        late(last, 0, C)
+        close(second)
+        close(third)
+        send_back(first, y_first[:])
+        rest = keep.tile([P, E - 1, C], F32, name="rest", tag="results")
 
         def relu(e):
-            nc.vector.tensor_scalar(rest[:, (e - 1) * C : e * C], banks[e][:], bias[:, e : e + 1], 0.0, ADD, MAX)
+            nc.vector.tensor_scalar(rest[:, e - 1, :], banks[e][:], bias[:, e : e + 1], 0.0, ADD, MAX)
 
-        relu(1)
-        close(2)
-        relu(3)
-        send_back(1, rest[:, :C])
-        send_back(2, rest[:, SCALAR_SCATTERS[2][0] - C :])
-        relu(2)
-        lo, hi = VECTOR_SCATTER
-        window = routed_v[:].indirect(offsets_of(lo, hi))
-        nc.vector.tensor_tensor(window, rest[:, lo - C : hi - C], gates[:, lo:hi], MULT)
+        relu(second)
+        close(last)
+        relu(third)
+        send_back(second, rest[:, second - 1, :])
+        relu(last)
+        send_back(third, rest[:, third - 1, :])
+        window = routed_v[:].indirect(offsets_of(last))
+        nc.vector.tensor_tensor(window, rest[:, last - 1, :], gates[:, last * C : (last + 1) * C], MULT)
         nc.vector.tensor_tensor(partial[:], routed_v[:], resid[:], ADD)
         for i, (lo, hi) in enumerate(CUTS):
             nc.vector.tensor_tensor(sums[i][:], routed_s[:, lo:hi], partial[:, lo:hi], ADD)

@@ -37,6 +37,11 @@ GPSIMD_WEAVES = ((0, 192), (192, HALF))
 VECTOR_WEAVE = (HALF, S)
 
 ORDER = (0, 2, 3, 1)
+SPLIT = 736
+QUARTER = C // 4
+EARLY_PIECES = ((0, C // 2, S), (C // 2, C // 2, S + C // 2), (2 * C, C, S + C + 3 * QUARTER), (3 * C, C // 2, S + 2 * C + 3 * QUARTER))
+HELD_PIECES = ((3 * C + C // 2, C // 2, S + QUARTER), (C, C, S + 3 * QUARTER))
+PICKED_WORDS = max(2 * at - lo for lo, slots, at in EARLY_PIECES + HELD_PIECES)
 CUT = 256
 CUTS = tuple((lo, lo + CUT) for lo in range(0, T, CUT))
 
@@ -57,7 +62,7 @@ def tile_moe_res_lin_relu_kernel(
         raw0 = keep.tile([P, 2, T], F32, name="raw0", align_bytes=64)
         raws = [[raw0[:, :, : T // 2], raw0[:, :, T // 2 :]]] + raws
         pairs = [keep.tile([P, T, 2], BF16, name=f"pairs{u}", align_bytes=64) for u in range(4)]
-        picked1 = keep.tile([P, 7, C], U32, name="picked1", align_bytes=64)
+        picked1 = keep.tile([P, PICKED_WORDS], U32, name="picked1", align_bytes=64)
         picked0 = keep.tile([P, 2, S], U32, name="picked0", align_bytes=64)
         woven0 = keep.tile([P, S, 2], U32, name="woven0", align_bytes=64)
         woven1 = {e: keep.tile([P, C, 2], U32, name=f"woven1_{e}", align_bytes=64)[:] for e in ORDER[:3]}
@@ -74,10 +79,9 @@ def tile_moe_res_lin_relu_kernel(
         bias = woven_last[:, 2 * C - 1 :].bitcast(F32)
         gates = keep.tile([P, S], F32, name="gates")
         resid = keep.tile([P, T], F32, name="resid")
-        gated = {e: keep.tile([P, C], F32, name=f"gated{e}") for e in ORDER[:3]}
+        gated = {e: keep.tile([P, SPLIT - HALF if e == 2 else C], F32, name=f"gated{e}") for e in (0, 1, 2)}
         routed_s = keep.tile([P, T], F32, name="routed_s")
         routed_v = keep.tile([P, T], F32, name="routed_v")
-        partial = keep.tile([P, T], F32, name="partial")
         sums = [keep.tile([P, hi - lo], F32, name=f"sum{i}") for i, (lo, hi) in enumerate(CUTS)]
         banks = [psum.tile([P, C], F32, name=f"bank{e}") for e in range(E)]
 
@@ -170,19 +174,17 @@ def tile_moe_res_lin_relu_kernel(
         for lo in (0, HALF):
             quantise(codes0[:, lo : lo + HALF], scales0[:, lo : lo + HALF], woven0[:, lo : lo + HALF, :])
 
-        blocks = (picked1[:, 0:3:2, :], picked1[:, 1:3, :], picked1[:, 3:6:2, :], picked1[:, 4:7:2, :])
         round_pair(2)
-        for half in range(2):
-            early = picked1[:, 3 * half : 3 * half + 2, :].rearrange("p e c -> p (e c)")
-            gather(early, 2, half * HALF, (half + 1) * HALF)
+        gather(picked1[:, :S], 2, 0, S)
         round_pair(3)
 
-        def offsets_of(e):
-            return offsets[:, e * C // LIST : (e + 1) * C // LIST]
+        def offsets_of(lo, hi):
+            return offsets[:, lo // LIST : hi // LIST]
 
-        def late(e, lo, hi):
-            gather(blocks[e][:, 1, lo:hi], 3, e * C + lo, e * C + hi)
-            nc.scalar.copy(woven1[e][:, lo:hi, :], side_by_side(blocks[e][:, :, lo:hi]))
+        def late(lo, slots, at):
+            gather(picked1[:, at : at + slots], 3, lo, lo + slots)
+            two_rows = picked1[:, lo : 2 * at - lo].rearrange("p (j c) -> p j c", j=2)[:, :, :slots]
+            nc.scalar.copy(woven1[lo // C][:, lo % C : lo % C + slots, :], side_by_side(two_rows))
 
         def close(e):
             quantise(codes1[e][:], scales1[e][:], woven1[e])
@@ -190,35 +192,38 @@ def tile_moe_res_lin_relu_kernel(
             product(e, 1)
 
         def send_back(e, results):
-            nc.vector.tensor_tensor(gated[e][:], results, gates[:, e * C : (e + 1) * C], MULT)
-            nc.scalar.activation(routed_s[:].indirect(offsets_of(e)), gated[e][:], COPY)
+            lo, hi = e * C, e * C + gated[e].shape[1]
+            nc.vector.tensor_tensor(gated[e][:], results, gates[:, lo:hi], MULT)
+            nc.scalar.activation(routed_s[:].indirect(offsets_of(lo, hi)), gated[e][:], COPY)
 
         first, second, third, last = ORDER
-        late(first, 0, C // 2)
-        late(first, C // 2, C)
-        late(second, 0, C)
-        late(third, 0, C)
+        for piece in EARLY_PIECES:
+            late(*piece)
         close(first)
+        late(*HELD_PIECES[0])
         y_first = keep.tile([P, C], F32, name="y_first", tag="results")
         nc.scalar.activation(y_first[:], banks[first][:], RELU, bias=bias[:, first : first + 1])
-        late(last, 0, C)
+        late(*HELD_PIECES[1])
         close(second)
         close(third)
         send_back(first, y_first[:])
-        rest = keep.tile([P, E - 1, C], F32, name="rest", tag="results")
+        upper = keep.tile([P, HALF], F32, name="upper", tag="results")
 
-        def relu(e):
-            nc.vector.tensor_scalar(rest[:, e - 1, :], banks[e][:], bias[:, e : e + 1], 0.0, ADD, MAX)
+        def relu(results, e):
+            nc.vector.tensor_scalar(results, banks[e][:], bias[:, e : e + 1], 0.0, ADD, MAX)
 
-        relu(second)
+        relu(upper[:, :C], second)
         close(last)
-        relu(third)
-        send_back(second, rest[:, second - 1, :])
-        relu(last)
-        send_back(third, rest[:, third - 1, :])
-        window = routed_v[:].indirect(offsets_of(last))
-        nc.vector.tensor_tensor(window, rest[:, last - 1, :], gates[:, last * C : (last + 1) * C], MULT)
-        nc.vector.tensor_tensor(partial[:], routed_v[:], resid[:], ADD)
+        relu(upper[:, C:], third)
+        y_last = keep.tile([P, C], F32, name="y_last", tag="last results")
+        nc.scalar.activation(y_last[:], banks[last][:], RELU, bias=bias[:, last : last + 1])
+        send_back(second, upper[:, : SPLIT - HALF])
+        window = routed_v[:].indirect(offsets_of(SPLIT, S))
+        nc.vector.tensor_tensor(window, upper[:, SPLIT - HALF :], gates[:, SPLIT:], MULT)
+        send_back(last, y_last[:])
+        partial = keep.tile([P, T], F32, name="partial", tag="last results")
+        for lo, hi in ((0, T // 2), (T // 2, T)):
+            nc.vector.tensor_tensor(partial[:, lo:hi], routed_v[:, lo:hi], resid[:, lo:hi], ADD)
         for i, (lo, hi) in enumerate(CUTS):
             nc.vector.tensor_tensor(sums[i][:], routed_s[:, lo:hi], partial[:, lo:hi], ADD)
             nc.sync.dma_start(out[:, lo:hi], sums[i][:])

@@ -36,11 +36,13 @@ HALF = S // 2
 GPSIMD_WEAVES = ((0, 192), (192, HALF))
 VECTOR_WEAVE = (HALF, S)
 
-ORDER = (0, 2, 3, 1)
-SPLIT = 736
+HALF_C = C // 2
+LAST = E - 1
+VECTOR_FROM = 2 * C
+VECTOR_TO = S - T // 8
 QUARTER = C // 4
-EARLY_PIECES = ((0, C // 2, S), (C // 2, C // 2, S + C // 2), (2 * C, C, S + C + 3 * QUARTER), (3 * C, C // 2, S + 2 * C + 3 * QUARTER))
-HELD_PIECES = ((3 * C + C // 2, C // 2, S + QUARTER), (C, C, S + 3 * QUARTER))
+EARLY_PIECES = ((0, HALF_C, S), (HALF_C, HALF_C, S + HALF_C), (C, C, S + C + 3 * QUARTER), (2 * C, HALF_C, S + 2 * C + 3 * QUARTER))
+HELD_PIECES = ((2 * C + HALF_C, HALF_C, S + QUARTER), (3 * C, C, S + 3 * QUARTER))
 PICKED_WORDS = max(2 * at - lo for lo, slots, at in EARLY_PIECES + HELD_PIECES)
 CUT = 256
 CUTS = tuple((lo, lo + CUT) for lo in range(0, T, CUT))
@@ -65,9 +67,9 @@ def tile_moe_res_lin_relu_kernel(
         picked1 = keep.tile([P, PICKED_WORDS], U32, name="picked1", align_bytes=64)
         picked0 = keep.tile([P, 2, S], U32, name="picked0", align_bytes=64)
         woven0 = keep.tile([P, S, 2], U32, name="woven0", align_bytes=64)
-        woven1 = {e: keep.tile([P, C, 2], U32, name=f"woven1_{e}", align_bytes=64)[:] for e in ORDER[:3]}
-        woven_last = keep.tile([P, 2 * C + E - 1], U32, name="woven_last", align_bytes=64)
-        woven1[1] = woven_last[:, : 2 * C].rearrange("p (s h) -> p s h", h=2)
+        woven1 = [keep.tile([P, C, 2], U32, name=f"woven1_{e}", align_bytes=64)[:] for e in range(LAST)]
+        tail = keep.tile([P, 2 * C + E - 2 + T // 2], U32, name="tail", align_bytes=64)
+        woven1.append(tail[:, : 2 * C].rearrange("p (s h) -> p s h", h=2))
         codes0 = keep.tile([P, S], U32, name="codes0", align_bytes=64)
         scales0 = keep.tile([P, S], U8, name="scales0", align_bytes=64)
         codes1 = [keep.tile([P, C], U32, name=f"codes1_{e}", align_bytes=64) for e in range(E)]
@@ -76,14 +78,15 @@ def tile_moe_res_lin_relu_kernel(
         w4 = keep.tile([P, E, 2 * N], U8, name="w4", align_bytes=64)
         w8_rows = keep.tile([P, E, N], U8, name="w8_rows", align_bytes=64)
         w4_rows = keep.tile([P, E, N], U8, name="w4_rows", align_bytes=64)
-        bias = woven_last[:, 2 * C - 1 :].bitcast(F32)
+        bias = tail[:, 2 * C - 1 : 2 * C - 1 + E].bitcast(F32)
+        bias_copy = tail[:, C - 1 : C].bitcast(F32)
         gates = keep.tile([P, S], F32, name="gates")
         resid = keep.tile([P, T], F32, name="resid")
-        gated = {e: keep.tile([P, SPLIT - HALF if e == 2 else C], F32, name=f"gated{e}") for e in (0, 1, 2)}
         routed_s = keep.tile([P, T], F32, name="routed_s")
         routed_v = keep.tile([P, T], F32, name="routed_v")
         sums = [keep.tile([P, hi - lo], F32, name=f"sum{i}") for i, (lo, hi) in enumerate(CUTS)]
-        banks = [psum.tile([P, C], F32, name=f"bank{e}") for e in range(E)]
+        groups = [(e * C, C) for e in range(LAST)] + [(LAST * C, HALF_C), (LAST * C + HALF_C, HALF_C)]
+        banks = [psum.tile([P, slots], F32, name=f"bank{g}") for g, (lo, slots) in enumerate(groups)]
 
         for rows in (w8_rows, w4_rows):
             nc.gpsimd.memset(rows[:].rearrange("p e n -> p (e n)").bitcast(I32), 0)
@@ -151,14 +154,17 @@ def tile_moe_res_lin_relu_kernel(
                 in_=woven.rearrange("p s h -> p (s h)").bitcast(BF16),
             )
 
-        def product(e, a):
-            slots = slice(e * C, (e + 1) * C)
+        def product(g, a):
+            lo, count = groups[g]
+            e = lo // C
+            slots = slice(lo, lo + count)
+            own = slice(lo % C, lo % C + count)
             nc.tensor.matmul_mx(
-                out=banks[e][:],
+                out=banks[g][:],
                 lhsT=w8[:, e, :].bitcast(FP8X4) if a == 0 else w4[:, e, :].bitcast(FP4X4),
                 lhsT_scale=(w8_rows, w4_rows)[a][:, e, :],
-                rhs=(codes0[:, slots] if a == 0 else codes1[e][:]).bitcast(FP8X4),
-                rhs_scale=scales0[:, slots] if a == 0 else scales1[e][:],
+                rhs=(codes0[:, slots] if a == 0 else codes1[e][:, own]).bitcast(FP8X4),
+                rhs_scale=scales0[:, slots] if a == 0 else scales1[e][:, own],
                 start=a == 0,
                 stop=a == 1,
             )
@@ -181,49 +187,68 @@ def tile_moe_res_lin_relu_kernel(
         def offsets_of(lo, hi):
             return offsets[:, lo // LIST : hi // LIST]
 
-        def late(lo, slots, at):
-            gather(picked1[:, at : at + slots], 3, lo, lo + slots)
+        def weave1(lo, slots, at):
             two_rows = picked1[:, lo : 2 * at - lo].rearrange("p (j c) -> p j c", j=2)[:, :, :slots]
             nc.scalar.copy(woven1[lo // C][:, lo % C : lo % C + slots, :], side_by_side(two_rows))
 
-        def close(e):
-            quantise(codes1[e][:], scales1[e][:], woven1[e])
-            product(e, 0)
-            product(e, 1)
+        def late(lo, slots, at):
+            gather(picked1[:, at : at + slots], 3, lo, lo + slots)
+            weave1(lo, slots, at)
 
-        def send_back(e, results):
-            lo, hi = e * C, e * C + gated[e].shape[1]
-            nc.vector.tensor_tensor(gated[e][:], results, gates[:, lo:hi], MULT)
-            nc.scalar.activation(routed_s[:].indirect(offsets_of(lo, hi)), gated[e][:], COPY)
+        def close(g):
+            lo, count = groups[g]
+            e, own = lo // C, slice(lo % C, lo % C + count)
+            quantise(codes1[e][:, own], scales1[e][:, own], woven1[e][:, own, :])
+            product(g, 0)
+            product(g, 1)
 
-        first, second, third, last = ORDER
+        def send_back(gated, results, lo, hi):
+            nc.vector.tensor_tensor(gated, results, gates[:, lo:hi], MULT)
+            nc.scalar.activation(routed_s[:].indirect(offsets_of(lo, hi)), gated, COPY)
+
         for piece in EARLY_PIECES:
             late(*piece)
-        close(first)
+        close(0)
         late(*HELD_PIECES[0])
+        nc.gpsimd.tensor_copy(bias_copy, bias[:, :1])
         y_first = keep.tile([P, C], F32, name="y_first", tag="results")
-        nc.scalar.activation(y_first[:], banks[first][:], RELU, bias=bias[:, first : first + 1])
-        late(*HELD_PIECES[1])
-        close(second)
-        close(third)
-        send_back(first, y_first[:])
-        upper = keep.tile([P, HALF], F32, name="upper", tag="results")
+        nc.scalar.activation(y_first[:, :HALF_C], banks[0][:, :HALF_C], RELU, bias=bias_copy)
+        nc.scalar.activation(y_first[:, HALF_C:], banks[0][:, HALF_C:], RELU, bias=bias[:, :1])
+        lo, slots, at = HELD_PIECES[1]
+        gather(picked1[:, at : at + slots], 3, lo, lo + slots)
+        for half in (0, HALF_C):
+            weave1(lo + half, HALF_C, at + half)
+        close(1)
+        close(2)
+        gated_first = keep.tile([P, C], F32, name="gated_first")
+        send_back(gated_first[:], y_first[:], 0, C)
+        later = keep.tile([P, S - C], F32, name="later", tag="results")
 
-        def relu(results, e):
-            nc.vector.tensor_scalar(results, banks[e][:], bias[:, e : e + 1], 0.0, ADD, MAX)
+        def results(lo, hi):
+            return later[:, lo - C : hi - C]
 
-        relu(upper[:, :C], second)
-        close(last)
-        relu(upper[:, C:], third)
-        y_last = keep.tile([P, C], F32, name="y_last", tag="last results")
-        nc.scalar.activation(y_last[:], banks[last][:], RELU, bias=bias[:, last : last + 1])
-        send_back(second, upper[:, : SPLIT - HALF])
-        window = routed_v[:].indirect(offsets_of(SPLIT, S))
-        nc.vector.tensor_tensor(window, upper[:, SPLIT - HALF :], gates[:, SPLIT:], MULT)
-        send_back(last, y_last[:])
-        partial = keep.tile([P, T], F32, name="partial", tag="last results")
-        for lo, hi in ((0, T // 2), (T // 2, T)):
-            nc.vector.tensor_tensor(partial[:, lo:hi], routed_v[:, lo:hi], resid[:, lo:hi], ADD)
+        def relu(g):
+            lo, count = groups[g]
+            nc.vector.tensor_scalar(results(lo, lo + count), banks[g][:], bias[:, lo // C : lo // C + 1], 0.0, ADD, MAX)
+
+        close(3)
+        relu(1)
+        close(4)
+        relu(2)
+        relu(3)
+        nc.scalar.activation(results(S - HALF_C, S), banks[4][:], RELU, bias=bias[:, LAST:])
+        gated_second = keep.tile([P, C], F32, name="gated_second", tag="second")
+        send_back(gated_second[:], results(C, 2 * C), C, 2 * C)
+        window = routed_v[:].indirect(offsets_of(VECTOR_FROM, VECTOR_TO))
+        nc.vector.tensor_tensor(window, results(VECTOR_FROM, VECTOR_TO), gates[:, VECTOR_FROM:VECTOR_TO], MULT)
+        gated_last = keep.tile([P, S - VECTOR_TO], F32, name="gated_last")
+        send_back(gated_last[:], results(VECTOR_TO, S), VECTOR_TO, S)
+        second_half = keep.tile([P, T // 2], F32, name="second_half", tag="second")
+        partial = (tail[:, 2 * C + E - 2 :].bitcast(F32), second_half[:])
+        for half in range(2):
+            tokens = slice(half * T // 2, (half + 1) * T // 2)
+            nc.vector.tensor_tensor(partial[half], routed_v[:, tokens], resid[:, tokens], ADD)
         for i, (lo, hi) in enumerate(CUTS):
-            nc.vector.tensor_tensor(sums[i][:], routed_s[:, lo:hi], partial[:, lo:hi], ADD)
+            half, start = divmod(lo, T // 2)
+            nc.vector.tensor_tensor(sums[i][:], routed_s[:, lo:hi], partial[half][:, start : start + hi - lo], ADD)
             nc.sync.dma_start(out[:, lo:hi], sums[i][:])

from contextlib import ExitStack

import concourse.mybir as mybir

F32 = mybir.dt.float32
BF16 = mybir.dt.bfloat16
I32 = mybir.dt.int32
U32 = mybir.dt.uint32
U16 = mybir.dt.uint16
U8 = mybir.dt.uint8
FP8X4 = mybir.dt.float8_e4m3fn_x4
FP4X4 = mybir.dt.float4_e2m1fn_x4
MULT = mybir.AluOpType.mult
ADD = mybir.AluOpType.add
COPY = mybir.ActivationFunctionType.Copy
RELU = mybir.ActivationFunctionType.Relu
MAX = mybir.AluOpType.max

P = 128
K, T, E, C, N = 1024, 1536, 4, 256, 128
S = E * C
PASS = 512
LIST = 16
FLOPS = 2 * E * C * K * N

PIECES = (
    ((768, "vector"), (768, "vector")),
    ((896, "gpsimd"), (640, "vector")),
    ((768, "none"), (768, "none")),
    ((768, "idle gpsimd"), (512, "gpsimd"), (256, "gpsimd")),
)
SCALAR_SHARE = {"vector": 9, "gpsimd": 16, "idle gpsimd": 13, "none": 24}
SHARE_STEP = 16

HALF = S // 2
GPSIMD_WEAVES = ((0, 192), (192, HALF))
VECTOR_WEAVE = (HALF, S)

HALF_C = C // 2
LAST = E - 1
VECTOR_FROM = 2 * C
VECTOR_TO = S - T // 8
QUARTER = C // 4
EARLY_PIECES = ((0, HALF_C, S), (HALF_C, HALF_C, S + HALF_C), (C, C, S + C + 3 * QUARTER), (2 * C, HALF_C, S + 2 * C + 3 * QUARTER))
HELD_PIECES = ((2 * C + HALF_C, HALF_C, S + QUARTER), (3 * C, C, S + 3 * QUARTER))
PICKED_WORDS = max(2 * at - lo for lo, slots, at in EARLY_PIECES + HELD_PIECES)
CUT = 256
CUTS = tuple((lo, lo + CUT) for lo in range(0, T, CUT))


def tile_moe_res_lin_relu_kernel(
    tc, xT, xr, w8_words, w8_scales, w4_words, w4_scales, b, gate, offs, out
):
    nc = tc.nc
    with ExitStack() as ctx:
        keep = ctx.enter_context(tc.tile_pool(name="keep", bufs=1))
        psum = ctx.enter_context(tc.psum_pool(name="psum", bufs=1))

        offsets = keep.tile([P, S // LIST], U16, name="offsets")
        raws = [
            [keep.tile([P, 2, tokens], F32, name=f"raw{u}_{i}", align_bytes=64) for i, (tokens, helper) in enumerate(PIECES[u])]
            for u in range(1, 4)
        ]
        raw0 = keep.tile([P, 2, T], F32, name="raw0", align_bytes=64)
        raws = [[raw0[:, :, : T // 2], raw0[:, :, T // 2 :]]] + raws
        pairs = [keep.tile([P, T, 2], BF16, name=f"pairs{u}", align_bytes=64) for u in range(4)]
        picked1 = keep.tile([P, PICKED_WORDS], U32, name="picked1", align_bytes=64)
        picked0 = keep.tile([P, 2, S], U32, name="picked0", align_bytes=64)
        woven0 = keep.tile([P, S, 2], U32, name="woven0", align_bytes=64)
        woven1 = [keep.tile([P, C, 2], U32, name=f"woven1_{e}", align_bytes=64)[:] for e in range(LAST)]
        tail = keep.tile([P, 2 * C + E - 2 + T // 2], U32, name="tail", align_bytes=64)
        woven1.append(tail[:, : 2 * C].rearrange("p (s h) -> p s h", h=2))
        codes0 = keep.tile([P, S], U32, name="codes0", align_bytes=64)
        scales0 = keep.tile([P, S], U8, name="scales0", align_bytes=64)
        codes1 = [keep.tile([P, C], U32, name=f"codes1_{e}", align_bytes=64) for e in range(E)]
        scales1 = [keep.tile([P, C], U8, name=f"scales1_{e}", align_bytes=64) for e in range(E)]
        w8 = keep.tile([P, E, 4 * N], U8, name="w8", align_bytes=64)
        w4 = keep.tile([P, E, 2 * N], U8, name="w4", align_bytes=64)
        w8_rows = keep.tile([P, E, N], U8, name="w8_rows", align_bytes=64)
        w4_rows = keep.tile([P, E, N], U8, name="w4_rows", align_bytes=64)
        bias = tail[:, 2 * C - 1 : 2 * C - 1 + E].bitcast(F32)
        bias_copy = tail[:, C - 1 : C].bitcast(F32)
        gates = keep.tile([P, S], F32, name="gates")
        resid = keep.tile([P, T], F32, name="resid")
        routed_s = keep.tile([P, T], F32, name="routed_s")
        routed_v = keep.tile([P, T], F32, name="routed_v")
        sums = [keep.tile([P, hi - lo], F32, name=f"sum{i}") for i, (lo, hi) in enumerate(CUTS)]
        groups = [(e * C, C) for e in range(LAST)] + [(LAST * C, HALF_C), (LAST * C + HALF_C, HALF_C)]
        banks = [psum.tile([P, slots], F32, name=f"bank{g}") for g, (lo, slots) in enumerate(groups)]

        for rows in (w8_rows, w4_rows):
            nc.gpsimd.memset(rows[:].rearrange("p e n -> p (e n)").bitcast(I32), 0)
        nc.vector.memset(routed_s[:, : T // 2], 0.0)
        nc.scalar.activation(routed_s[:, T // 2 :], routed_s[:, : T // 2], COPY)
        nc.vector.memset(routed_v[:], 0.0)

        def first_token(u, i):
            return sum(tokens for tokens, helper in PIECES[u][:i])

        def load_x(u, i):
            a, h = divmod(u, 2)
            start = first_token(u, i)
            rows = xT[PASS * a : PASS * (a + 1), start : start + PIECES[u][i][0]].rearrange("(p t) w -> p t w", t=4)
            nc.sync.dma_start(raws[u][i][:], rows[:, 2 * h : 2 * h + 2, :])

        def load_scale_rows(rows, scales):
            for quadrant in range(4):
                nc.sync.dma_start(
                    rows[32 * quadrant : 32 * quadrant + 4, :, :].bitcast(I32),
                    scales[:, 0, 4 * quadrant : 4 * quadrant + 4, :].rearrange("e q n -> q e n").bitcast(I32),
                )

        first_rows = xT[:PASS, :].rearrange("(p t) w -> p (t w)", t=4)
        raw0_rows = raw0[:].rearrange("p j c -> p (j c)")
        joint = T + PIECES[0][0][0]
        nc.sync.dma_start(raw0_rows[:, :joint], first_rows[:, :joint])
        nc.sync.dma_start(raw0_rows[:, joint:], first_rows[:, joint : 2 * T])
        nc.sync.dma_start(offsets[:], offs)
        for u in range(1, 4):
            for i in range(len(PIECES[u])):
                load_x(u, i)
        load_scale_rows(w4_rows, w4_scales)
        nc.sync.dma_start(w4[:].bitcast(I32), w4_words.rearrange("e a p m -> p (e a) m").bitcast(I32))
        nc.sync.dma_start(w8[:].bitcast(I32), w8_words.rearrange("e a p n t -> p (e a) (n t)").bitcast(I32))
        nc.sync.dma_start(gates[:, :C], gate[:, :C])
        load_scale_rows(w8_rows, w8_scales)
        nc.sync.dma_start(bias, b)
        nc.sync.dma_start(gates[:, C:], gate[:, C:])
        nc.sync.dma_start(resid[:], xr)

        def side_by_side(two_rows):
            return two_rows.rearrange("p j c -> p c j")

        def round_pair(u):
            for i, (tokens, helper) in enumerate(PIECES[u]):
                start = first_token(u, i)
                share = round(tokens * SCALAR_SHARE[helper] / 24 / SHARE_STEP) * SHARE_STEP
                nc.scalar.activation(pairs[u][:, start : start + share, :], side_by_side(raws[u][i][:, :, :share]), COPY)
                if helper != "none":
                    engine = nc.vector if helper == "vector" else nc.gpsimd
                    engine.tensor_copy(pairs[u][:, start + share : start + tokens, :], side_by_side(raws[u][i][:, :, share:]))

        def gather(picked, u, lo, hi):
            window = pairs[u][:].rearrange("p t j -> p (t j)").bitcast(U32)
            nc.vector.tensor_copy(picked, window.indirect(offsets[:, lo // LIST : hi // LIST]))

        def weave0(engine, lo, hi):
            engine.tensor_copy(woven0[:, lo:hi, :].bitcast(I32), side_by_side(picked0[:, :, lo:hi].bitcast(I32)))

        def quantise(codes, scales, woven):
            nc.vector.quantize_mx(
                out=codes.bitcast(FP8X4),
                scales=scales,
                in_=woven.rearrange("p s h -> p (s h)").bitcast(BF16),
            )

        def product(g, a):
            lo, count = groups[g]
            e = lo // C
            slots = slice(lo, lo + count)
            own = slice(lo % C, lo % C + count)
            nc.tensor.matmul_mx(
                out=banks[g][:],
                lhsT=w8[:, e, :].bitcast(FP8X4) if a == 0 else w4[:, e, :].bitcast(FP4X4),
                lhsT_scale=(w8_rows, w4_rows)[a][:, e, :],
                rhs=(codes0[:, slots] if a == 0 else codes1[e][:, own]).bitcast(FP8X4),
                rhs_scale=scales0[:, slots] if a == 0 else scales1[e][:, own],
                start=a == 0,
                stop=a == 1,
            )

        round_pair(0)
        gather(picked0[:, 0, :], 0, 0, S)
        round_pair(1)
        for lo, hi in GPSIMD_WEAVES + (VECTOR_WEAVE,):
            gather(picked0[:, 1, lo:hi], 1, lo, hi)
        for lo, hi in GPSIMD_WEAVES:
            weave0(nc.gpsimd, lo, hi)
        weave0(nc.vector, *VECTOR_WEAVE)
        for lo in (0, HALF):
            quantise(codes0[:, lo : lo + HALF], scales0[:, lo : lo + HALF], woven0[:, lo : lo + HALF, :])

        round_pair(2)
        gather(picked1[:, :S], 2, 0, S)
        round_pair(3)

        def offsets_of(lo, hi):
            return offsets[:, lo // LIST : hi // LIST]

        def weave1(lo, slots, at):
            two_rows = picked1[:, lo : 2 * at - lo].rearrange("p (j c) -> p j c", j=2)[:, :, :slots]
            nc.scalar.copy(woven1[lo // C][:, lo % C : lo % C + slots, :], side_by_side(two_rows))

        def late(lo, slots, at):
            gather(picked1[:, at : at + slots], 3, lo, lo + slots)
            weave1(lo, slots, at)

        def close(g):
            lo, count = groups[g]
            e, own = lo // C, slice(lo % C, lo % C + count)
            quantise(codes1[e][:, own], scales1[e][:, own], woven1[e][:, own, :])
            product(g, 0)
            product(g, 1)

        def send_back(gated, results, lo, hi):
            nc.vector.tensor_tensor(gated, results, gates[:, lo:hi], MULT)
            nc.scalar.activation(routed_s[:].indirect(offsets_of(lo, hi)), gated, COPY)

        for piece in EARLY_PIECES:
            late(*piece)
        close(0)
        late(*HELD_PIECES[0])
        nc.gpsimd.tensor_copy(bias_copy, bias[:, :1])
        y_first = keep.tile([P, C], F32, name="y_first", tag="results")
        nc.scalar.activation(y_first[:, :HALF_C], banks[0][:, :HALF_C], RELU, bias=bias_copy)
        nc.scalar.activation(y_first[:, HALF_C:], banks[0][:, HALF_C:], RELU, bias=bias[:, :1])
        lo, slots, at = HELD_PIECES[1]
        gather(picked1[:, at : at + slots], 3, lo, lo + slots)
        for half in (0, HALF_C):
            weave1(lo + half, HALF_C, at + half)
        close(1)
        close(2)
        gated_first = keep.tile([P, C], F32, name="gated_first")
        send_back(gated_first[:], y_first[:], 0, C)
        later = keep.tile([P, S - C], F32, name="later", tag="results")

        def results(lo, hi):
            return later[:, lo - C : hi - C]

        def relu(g):
            lo, count = groups[g]
            nc.vector.tensor_scalar(results(lo, lo + count), banks[g][:], bias[:, lo // C : lo // C + 1], 0.0, ADD, MAX)

        close(3)
        relu(1)
        close(4)
        relu(2)
        relu(3)
        nc.scalar.activation(results(S - HALF_C, S), banks[4][:], RELU, bias=bias[:, LAST:])
        gated_second = keep.tile([P, C], F32, name="gated_second", tag="second")
        send_back(gated_second[:], results(C, 2 * C), C, 2 * C)
        window = routed_v[:].indirect(offsets_of(VECTOR_FROM, VECTOR_TO))
        nc.vector.tensor_tensor(window, results(VECTOR_FROM, VECTOR_TO), gates[:, VECTOR_FROM:VECTOR_TO], MULT)
        gated_last = keep.tile([P, S - VECTOR_TO], F32, name="gated_last")
        send_back(gated_last[:], results(VECTOR_TO, S), VECTOR_TO, S)
        second_half = keep.tile([P, T // 2], F32, name="second_half", tag="second")
        partial = (tail[:, 2 * C + E - 2 :].bitcast(F32), second_half[:])
        for half in range(2):
            tokens = slice(half * T // 2, (half + 1) * T // 2)
            nc.vector.tensor_tensor(partial[half], routed_v[:, tokens], resid[:, tokens], ADD)
        for i, (lo, hi) in enumerate(CUTS):
            half, start = divmod(lo, T // 2)
            nc.vector.tensor_tensor(sums[i][:], routed_s[:, lo:hi], partial[half][:, start : start + hi - lo], ADD)
            nc.sync.dma_start(out[:, lo:hi], sums[i][:])
